import numpy as np
import ml_dtypes


def mxq(x, axis, fmt="e4m3"):
    dtype, down = {"e4m3": (ml_dtypes.float8_e4m3fn, 7), "e5m2": (ml_dtypes.float8_e5m2, 14)}[fmt]
    v = np.moveaxis(np.asarray(x, np.float32).astype(ml_dtypes.bfloat16).astype(np.float64), axis, -1)
    blocks = v.reshape(v.shape[:-1] + (-1, 32))
    amax = np.abs(blocks).max(-1, keepdims=True)
    byte = np.maximum(np.where(amax > 0, np.frexp(amax)[1] - 1 + 127, 0) - down, 1)
    scale = np.exp2(byte - 127.0)
    codes = (blocks / scale).astype(np.float32).astype(dtype).astype(np.float64)
    return np.moveaxis((codes * scale).reshape(v.shape), -1, axis)


WIDE = False


def mx_kscale(k):
    if not WIDE:
        return np.ones(k)
    levels = np.array([24, -24, 12, -12, 0])
    if k % 512:
        return np.exp2(np.random.permutation(np.resize(levels, k // 32))).repeat(32)
    a = np.empty((k // 512, 16))
    for p in range(k // 512):
        a[p, :8] = np.random.permutation(np.resize(levels, 8))
        for g in range(8):
            far = levels[np.abs(levels - a[p, g]) >= 10]
            a[p, g + 8] = far[np.random.randint(len(far))]
    return np.exp2(a.ravel()).repeat(32)


def f64(x):
    return np.asarray(x).astype(np.float64)


def striped(idx):
    return np.tile(idx.reshape(-1, 16).T, (8, 1)).astype(np.uint16)


def unstriped(offs):
    return offs[:16].T.reshape(-1).astype(np.int64)


E2M1 = np.array([0.0, 0.5, 1.0, 1.5, 2.0, 3.0, 4.0, 6.0, -0.0, -0.5, -1.0, -1.5, -2.0, -3.0, -4.0, -6.0])


def pack_weight(w, fmt):
    k, n = w.shape
    w = f64(np.asarray(w, np.float32).astype(ml_dtypes.bfloat16)).reshape(k // 32, 32, n)
    amax = np.abs(w).max(1)
    if fmt == "e4m3":
        byte = np.frexp(amax)[1] - 1 + 127 - 7
    else:
        mant, ex = np.frexp(amax / 6.0)
        byte = np.where(mant > 0.5, ex, ex - 1) + 127
    byte = np.clip(np.where(amax > 0, byte, 1), 1, 254)
    scaled = (w * np.exp2(127.0 - byte)[:, None, :]).reshape(k, n).astype(np.float32)
    by_word = np.ascontiguousarray(scaled.reshape(k // 512, 128, 4, n).transpose(0, 1, 3, 2))
    if fmt == "e4m3":
        words = by_word.astype(ml_dtypes.float8_e4m3fn).view(np.uint8)
    else:
        c = by_word.astype(ml_dtypes.float4_e2m1fn).view(np.uint8) & 0xF
        words = (c[..., 0::2] | (c[..., 1::2] << 4)).reshape(k // 512, 128, 2 * n)
    return np.ascontiguousarray(words), np.ascontiguousarray(byte.astype(np.uint8).reshape(k // 512, 16, n))


def unpack_weight(words, scales, fmt):
    g, _, n = scales.shape
    words = np.ascontiguousarray(words).reshape(g, 128, n, -1)
    if fmt == "e4m3":
        vals = words.view(ml_dtypes.float8_e4m3fn).astype(np.float64)
    else:
        nib = np.empty((g, 128, n, 4), np.uint8)
        nib[..., 0::2] = words & 0xF
        nib[..., 1::2] = words >> 4
        vals = E2M1[nib]
    vals = vals * np.repeat(np.exp2(scales.astype(np.float64) - 127.0), 8, axis=1)[..., None]
    return vals.transpose(0, 1, 3, 2).reshape(g * 512, n)


def planes(y):
    n, m = y.shape
    v = y.astype(np.float32).astype(ml_dtypes.bfloat16).astype(np.float64).reshape(n // 32, 32, m)
    top = np.abs(v).max(1)
    byte = np.clip(np.where(top > 0, np.frexp(top)[1] - 1 + 127 - 7, 1), 1, 254)
    codes = (v * np.exp2(127.0 - byte)[:, None, :]).reshape(n, m).astype(np.float32).astype(ml_dtypes.float8_e4m3fn).view(np.uint8)
    words = codes.reshape(n // 512, 128, 4, m).transpose(0, 1, 3, 2)
    return np.ascontiguousarray(words), np.ascontiguousarray(byte.astype(np.uint8).reshape(n // 512, 16, m))


def gelu(f):
    return 0.5 * f * (1.0 + np.tanh(np.sqrt(2.0 / np.pi) * (f + 0.044715 * f**3)))


K, R, N, T, J = 512, 1024, 512, 2048, 1024


def setup_inputs():
    n = np.random.standard_normal
    s = mx_kscale(K)[:, None]
    u = mx_kscale(R)[:, None]
    wd = n((R, N)) / np.sqrt(R) / u
    p_tab = pack_weight(n((K, T)) * s, "e4m3")
    p_wu = pack_weight(n((K, R)) / np.sqrt(K) / s, "e2m1")
    p_wd8 = pack_weight(wd[:512], "e4m3")
    p_wd4 = pack_weight(wd[512:], "e2m1")
    return {
        "tab_words": p_tab[0],
        "tab_scales": p_tab[1],
        "wu_words": p_wu[0],
        "wu_scales": p_wu[1],
        "sm": (np.random.uniform(0.5, 2.0, R) * u[:, 0]).astype(np.float32),
        "wd8_words": p_wd8[0],
        "wd8_scales": p_wd8[1],
        "wd4_words": p_wd4[0],
        "wd4_scales": p_wd4[1],
        "rT": (n((N, T))).astype(np.float32),
        "wgo": np.tile(np.random.uniform(0.5, 2.0, J), (128, 1)).astype(np.float32),
        "offs": striped(np.random.permutation(T)[:J]),
    }


def reference(tab_words, tab_scales, wu_words, wu_scales, sm, wd8_words, wd8_scales, wd4_words, wd4_scales, rT, wgo, offs):
    idx = unstriped(offs)
    tab_ = unpack_weight(tab_words, tab_scales, "e4m3")[:, idx]
    wu_ = unpack_weight(wu_words, wu_scales, "e2m1")
    a = wu_.T @ tab_
    h = f64(sm)[:, None] * gelu(a)
    h_ = mxq(h, 0, "e4m3")
    wd8_ = unpack_weight(wd8_words, wd8_scales, "e4m3")
    wd4_ = unpack_weight(wd4_words, wd4_scales, "e2m1")
    y = wd8_.T @ h_[:512] + wd4_.T @ h_[512:]
    out = np.zeros((N, T))
    out[:, idx] = f64(wgo)[0] * (y + f64(rT)[:, idx])
    return (out,) + planes(out)

@@ -1,0 +1,270 @@
+from contextlib import ExitStack
+
+import concourse.mybir as mybir
+
+K, R, N, T, J = 512, 1024, 512, 2048, 1024
+FLOPS = 2 * K * R * J + 2 * R * N * J
+
+F32 = mybir.dt.float32
+BF16 = mybir.dt.bfloat16
+I32 = mybir.dt.int32
+U32 = mybir.dt.uint32
+U16 = mybir.dt.uint16
+U8 = mybir.dt.uint8
+E4M3 = mybir.dt.float8_e4m3fn_x4
+E2M1 = mybir.dt.float4_e2m1fn_x4
+GELU = mybir.ActivationFunctionType.Gelu_apprx_tanh
+COPY = mybir.ActivationFunctionType.Copy
+MULT = mybir.AluOpType.mult
+ADD = mybir.AluOpType.add
+
+P = 128
+CH = 256
+NCH = J // CH
+TAIL = (("v", 256), ("s", 256), ("v", 512), ("s", 512), ("v", 256), ("s", 256))
+
+
+def tile_list_modp_gelu_mix_resP_kernel(
+    tc, tab_words, tab_scales, wu_words, wu_scales, sm, wd8_words, wd8_scales, wd4_words, wd4_scales,
+    rT, wgo, offs, out_0, out_1, out_2
+):
+    nc = tc.nc
+    with ExitStack() as ctx:
+        lists = ctx.enter_context(tc.tile_pool(name="lists", bufs=1))
+        keep = ctx.enter_context(tc.tile_pool(name="keep", bufs=1))
+        ring = ctx.enter_context(tc.tile_pool(name="ring", bufs=2))
+        ps_up = ctx.enter_context(tc.psum_pool(name="ps_up", bufs=4))
+        ps_down = ctx.enter_context(tc.psum_pool(name="ps_down", bufs=4))
+
+        def kept(shape, dtype, name, tag=None):
+            return keep.tile(shape, dtype, name=name, tag=tag or name, align_bytes=64)
+
+        offsets = lists.tile([P, J // 16], U16, name="offsets")
+
+        def picks(c):
+            return offsets[:, c * CH // 16 : (c + 1) * CH // 16]
+
+        tab_sc = kept([P, T], U8, "tab_sc")
+        wu_sc_raw = kept([P, R], U8, "wu_sc_raw")
+        wd_sc_raw = kept([P, N], U8, "wd_sc_raw")
+        nc.vector.memset(tab_sc[:].bitcast(I32), 0)
+        nc.vector.memset(wu_sc_raw[:].bitcast(I32), 0)
+        nc.vector.memset(wd_sc_raw[:].bitcast(I32), 0)
+        pages = [None] * 4
+
+        warm = kept([P, 1], F32, "warm")
+        warm2 = kept([P, 1], F32, "warm2")
+        nc.gpsimd.memset(warm[:], 0.0)
+        nc.scalar.activation(warm2[:], warm[:], GELU)
+
+        def load_scale_rows(tile, first, rows, queues=(nc.sync,) * 4):
+            for q in range(4):
+                queues[q].dma_start(
+                    tile[32 * q + first : 32 * q + first + 4, :].bitcast(I32), rows[4 * q : 4 * q + 4, :].bitcast(I32)
+                )
+
+        tab_w = kept([P, T], U32, "tab_w")
+        wu_raw = kept([P, 2 * R], U8, "wu_raw")
+        wd8_raw = kept([P, N], I32, "wd8_raw")
+        wd4_raw = kept([P, 2 * N], U8, "wd4_raw")
+        sm_sb = kept([P, 2, 4], F32, "sm_sb")
+        wgo_sb = kept([P, J], F32, "wgo_sb")
+        nc.sync.dma_start(offsets[:], offs)
+        nc.sync.dma_start(wu_raw[:].bitcast(I32), wu_words[0].bitcast(I32))
+        nc.sync.dma_start(tab_w[:].bitcast(I32), tab_words[0].rearrange("p t i -> p (t i)").bitcast(I32))
+        load_scale_rows(tab_sc, 0, tab_scales[0])
+        load_scale_rows(wu_sc_raw, 0, wu_scales[0], (nc.sync, nc.sync, nc.sync, nc.gpsimd))
+        nc.gpsimd.dma_start(sm_sb[:], sm.rearrange("(a p t) -> p a t", a=2, t=4))
+        nc.sync.dma_start(wd8_raw[:], wd8_words[0].rearrange("p n i -> p (n i)").bitcast(I32))
+        nc.sync.dma_start(wd4_raw[:].bitcast(I32), wd4_words[0].bitcast(I32))
+        load_scale_rows(wd_sc_raw, 0, wd4_scales[0])
+        load_scale_rows(wd_sc_raw, 4, wd8_scales[0])
+        res = [kept([P, T], F32, "res%d" % t) for t in range(4)]
+        rT_by_plane = rT.rearrange("(p t) c -> p t c", t=4)
+        nc.sync.dma_start(res[0][:], rT_by_plane[:, 0, :])
+        nc.sync.dma_start(wgo_sb[:], wgo)
+        for t in range(1, 4):
+            nc.sync.dma_start(res[t][:], rT_by_plane[:, t, :])
+
+        def deal(dst, src):
+            nc.vector.tensor_copy(dst.rearrange("p (t m) -> p t m", t=4), src.rearrange("p (m t) -> p t m", t=4))
+
+        got_w = [None] * NCH
+        got_sc = [None] * NCH
+
+        def gather_table(c, tag_w=None, tag_sc=None):
+            got_sc[c] = kept([P, CH], U8, "got_sc%d" % c, tag_sc)
+            got_w[c] = kept([P, CH], U32, "got_w%d" % c, tag_w)
+            nc.vector.tensor_copy(got_sc[c][:], tab_sc[:].indirect(picks(c)))
+            nc.vector.tensor_copy(got_w[c][:], tab_w[:].indirect(picks(c)))
+
+        wu = [kept([P, 1024], U8, "wu%d" % a) for a in range(2)]
+        wu_sc = [kept([P, 512], U8, "wu_sc%d" % a) for a in range(2)]
+
+        def deal_wu(a):
+            deal(wu[a][:].bitcast(U16), wu_raw[:].bitcast(U16)[:, 512 * a : 512 * (a + 1)])
+            deal(wu_sc[a][:], wu_sc_raw[:, 512 * a : 512 * (a + 1)])
+
+        def up_matmul(out, c, a, t, cols):
+            nc.tensor.matmul_mx(
+                out, lhsT=wu[a][:, 256 * t : 256 * (t + 1)].bitcast(E2M1), lhsT_scale=wu_sc[a][:, P * t : P * (t + 1)],
+                rhs=got_w[c][:, cols].bitcast(E4M3), rhs_scale=got_sc[c][:, cols], start=True, stop=True,
+            )
+
+        h_in = [None] * NCH
+
+        def hidden_first():
+            h_in[0] = kept([P, 2, 2, P, 4], BF16, "h_in0")
+            for half in range(2):
+                for a in range(2):
+                    cols = slice(P * half, P * (half + 1))
+                    bank = ps_up.tile([P, 4, P], F32, name="up_bank", tag="up")
+                    for t in range(4):
+                        up_matmul(bank[:, t, :], 0, a, t, cols)
+                    act = kept([P, P, 4], F32, "act_first%d%d" % (a, half))
+                    nc.scalar.activation(act[:], bank[:].rearrange("p t j -> p j t"), GELU)
+                    nc.vector.tensor_tensor(
+                        h_in[0][:, half, a], act[:], sm_sb[:, a, :].unsqueeze(1).to_broadcast([P, P, 4]), MULT
+                    )
+
+        def hidden(c):
+            h_in[c] = kept([P, 2, CH, 4], BF16, "h_in%d" % c)
+            for a in range(2):
+                flat = ring.tile([P, 4, CH], BF16, name="flat", tag="flat")
+                for u in range(2):
+                    bank = ps_up.tile([P, 2, CH], F32, name="up_bank", tag="up")
+                    for e in range(2):
+                        up_matmul(bank[:, e, :], c, a, 2 * u + e, slice(0, CH))
+                    act = ring.tile([P, 2, CH], F32, name="act", tag="act")
+                    nc.scalar.activation(act[:], bank[:], GELU)
+                    for e in range(2):
+                        t = 2 * u + e
+                        nc.scalar.activation(flat[:, t, :], act[:, e, :], COPY, scale=sm_sb[:, a, t : t + 1])
+                nc.scalar.copy(
+                    h_in[c][:, a].rearrange("p (c i) t -> p c t i", i=4), flat[:].rearrange("p t (c i) -> p c t i", i=4)
+                )
+
+        wd8 = kept([P, N], I32, "wd8")
+        wd4 = kept([P, 2 * N], U8, "wd4")
+        wd_sc = kept([P, N], U8, "wd_sc")
+        y = [None] * NCH
+
+        def down(c):
+            h_w = ring.tile([P, 2, CH], U32, name="h_w", tag="h_w", align_bytes=64)
+            h_sc = ring.tile([P, 2, CH], U8, name="h_sc", tag="h_sc", align_bytes=64)
+            nc.vector.quantize_mx(
+                out=h_w[:].rearrange("p a j -> p (a j)").bitcast(E4M3),
+                scales=h_sc[:].rearrange("p a j -> p (a j)"),
+                in_=h_in[c][:].rearrange("p a j t -> p (a j t)"),
+            )
+            y[c] = [None] * 2
+            for u in range(2):
+                bank = ps_down.tile([P, 2, CH], F32, name="down_bank", tag="down")
+                for e in range(2):
+                    t = 2 * u + e
+                    for half in range(2):
+                        cols = slice(P * half, P * (half + 1))
+                        nc.tensor.matmul_mx(
+                            bank[:, e, cols], lhsT=wd8[:, P * t : P * (t + 1)].bitcast(E4M3),
+                            lhsT_scale=wd_sc[4:P, P * t : P * (t + 1)],
+                            rhs=h_w[:, 0, cols].bitcast(E4M3), rhs_scale=h_sc[:, 0, cols], start=True, stop=False,
+                        )
+                        nc.tensor.matmul_mx(
+                            bank[:, e, cols], lhsT=wd4[:, 256 * t : 256 * (t + 1)].bitcast(E2M1),
+                            lhsT_scale=wd_sc[:, P * t : P * (t + 1)],
+                            rhs=h_w[:, 1, cols].bitcast(E4M3), rhs_scale=h_sc[:, 1, cols], start=False, stop=True,
+                        )
+                y[c][u] = kept([P, 2, CH], F32, "y%d%d" % (c, u))
+                nc.scalar.copy(y[c][u][:], bank[:])
+
+        def down_first():
+            banks = [ps_down.tile([P, 2, CH], F32, name="down_bank", tag="down") for u in range(2)]
+            y[0] = [kept([P, 2, CH], F32, "y0%d" % u) for u in range(2)]
+            for half in range(2):
+                cols = slice(P * half, P * (half + 1))
+                h_w = kept([P, 2, P], U32, "h_w_first%d" % half)
+                h_sc = kept([P, 2, P], U8, "h_sc_first%d" % half)
+                nc.vector.quantize_mx(
+                    out=h_w[:].rearrange("p a j -> p (a j)").bitcast(E4M3),
+                    scales=h_sc[:].rearrange("p a j -> p (a j)"),
+                    in_=h_in[0][:, half].rearrange("p a j t -> p (a j t)"),
+                )
+                for t in range(4):
+                    out = banks[t // 2][:, t % 2, cols]
+                    nc.tensor.matmul_mx(
+                        out, lhsT=wd8[:, P * t : P * (t + 1)].bitcast(E4M3), lhsT_scale=wd_sc[4:P, P * t : P * (t + 1)],
+                        rhs=h_w[:, 0, :].bitcast(E4M3), rhs_scale=h_sc[:, 0, :], start=True, stop=False,
+                    )
+                    nc.tensor.matmul_mx(
+                        out, lhsT=wd4[:, 256 * t : 256 * (t + 1)].bitcast(E2M1), lhsT_scale=wd_sc[:, P * t : P * (t + 1)],
+                        rhs=h_w[:, 1, :].bitcast(E4M3), rhs_scale=h_sc[:, 1, :], start=False, stop=True,
+                    )
+                    if half == 1 and t % 2 == 1:
+                        nc.scalar.copy(y[0][t // 2][:], banks[t // 2][:])
+
+        def place(c, t, total):
+            nc.vector.tensor_tensor(total, res[t][:].indirect(picks(c)), y[c][t // 2][:, t % 2, :], ADD)
+            nc.vector.tensor_tensor(pages[t][:].indirect(picks(c)), total, wgo_sb[:, c * CH : (c + 1) * CH], MULT)
+
+        def fresh_total():
+            total = ring.tile([P, CH], F32, name="total", tag="total")
+            return total[:]
+
+        gather_table(0)
+        deal_wu(0)
+        deal_wu(1)
+        hidden_first()
+        deal(wd8[:], wd8_raw[:])
+        deal(wd4[:].bitcast(U16), wd4_raw[:].bitcast(U16))
+        deal(wd_sc[:], wd_sc_raw[:])
+        gather_table(1)
+        down_first()
+        gather_table(2, "act_first11", "act_first01")
+        gather_table(3, "act_first10", "act_first00")
+        for t in range(3):
+            pages[t] = kept([P, T], F32, "page%d" % t)
+            for half in range(2):
+                nc.vector.memset(pages[t][:, half * T // 2 : (half + 1) * T // 2], 0.0)
+        pages[3] = kept([P, T], F32, "page3", "h_in0")
+        nc.gpsimd.memset(pages[3][:], 0.0)
+
+        out_by_plane = out_0.rearrange("(p t) c -> p t c", t=4)
+        starts = [sum(w for e, w in TAIL[:k]) for k in range(len(TAIL))]
+        flat_out = [kept([P, 4, w], BF16, "flat_out%d" % k) for k, (e, w) in enumerate(TAIL)]
+
+        def finish_plane(t):
+            nc.sync.dma_start(out_by_plane[:, t, :], pages[t][:])
+            if t < 3:
+                for k, (e, w) in enumerate(TAIL):
+                    nc.scalar.copy(flat_out[k][:, t, :], pages[t][:, starts[k] : starts[k] + w])
+
+        for c in range(NCH):
+            last = c == NCH - 1
+            if not last:
+                hidden(c + 1)
+            for t in range(3):
+                place(c, t, fresh_total())
+                if last:
+                    finish_plane(t)
+            if last:
+                place(c, 3, fresh_total())
+                finish_plane(3)
+            else:
+                down(c + 1)
+                place(c, 3, h_in[c + 1][:].rearrange("p a j t -> p (a j t)").bitcast(F32)[:, 0:CH])
+
+        out_w = kept([P, T], U32, "out_w")
+        out_sc = kept([P, T], U8, "out_sc")
+        out_words = out_1[0].rearrange("p t i -> p (t i)").bitcast(I32)
+        for k, (e, w) in enumerate(TAIL):
+            cols = slice(starts[k], starts[k] + w)
+            copy = nc.vector.tensor_copy if e == "v" else nc.scalar.copy
+            woven = kept([P, w, 4], BF16, "woven%d" % k)
+            copy(flat_out[k][:, 3, :], pages[3][:, cols])
+            copy(woven[:].rearrange("p (c i) t -> p c t i", i=4), flat_out[k][:].rearrange("p t (c i) -> p c t i", i=4))
+            nc.vector.quantize_mx(
+                out=out_w[:, cols].bitcast(E4M3), scales=out_sc[:, cols], in_=woven[:].rearrange("p c t -> p (c t)")
+            )
+            nc.sync.dma_start(out_words[:, cols], out_w[:, cols].bitcast(I32))
+        for q in range(4):
+            nc.scalar.dma_start(out_2[0, 4 * q : 4 * q + 4, :].bitcast(I32), out_sc[32 * q : 32 * q + 4, :].bitcast(I32))

@@ -33,11 +33,17 @@ def tile_list_modp_gelu_mix_resP_kernel(
         lists = ctx.enter_context(tc.tile_pool(name="lists", bufs=1))
         keep = ctx.enter_context(tc.tile_pool(name="keep", bufs=1))
         ring = ctx.enter_context(tc.tile_pool(name="ring", bufs=2))
-        ps_up = ctx.enter_context(tc.psum_pool(name="ps_up", bufs=4))
-        ps_down = ctx.enter_context(tc.psum_pool(name="ps_down", bufs=4))
+        shared = ctx.enter_context(tc.tile_pool(name="shared", bufs=1))
+        psum = ctx.enter_context(tc.psum_pool(name="psum", bufs=1))
+
+        def bank_tile(shape, b):
+            return psum.tile(shape, F32, name="bank%d" % b, tag="bank%d" % b)
 
         def kept(shape, dtype, name, tag=None):
             return keep.tile(shape, dtype, name=name, tag=tag or name, align_bytes=64)
+
+        def laid(shape, dtype, name, offset):
+            return shared.tile(shape, dtype, name=name, tag=name, align_bytes=64, offset=offset)
 
         offsets = lists.tile([P, J // 16], U16, name="offsets")
 
@@ -46,9 +52,9 @@ def tile_list_modp_gelu_mix_resP_kernel(
 
         tab_sc = kept([P, T], U8, "tab_sc")
         wu_sc_raw = kept([P, R], U8, "wu_sc_raw")
-        wd_sc_raw = kept([P, N], U8, "wd_sc_raw")
-        nc.vector.memset(tab_sc[:].bitcast(I32), 0)
+        wd_sc_raw = laid([P, N], U8, "wd_sc_raw", 1024)
         nc.vector.memset(wu_sc_raw[:].bitcast(I32), 0)
+        nc.vector.memset(tab_sc[:].bitcast(I32), 0)
         nc.vector.memset(wd_sc_raw[:].bitcast(I32), 0)
         pages = [None] * 4
 
@@ -57,24 +63,24 @@ def tile_list_modp_gelu_mix_resP_kernel(
         nc.gpsimd.memset(warm[:], 0.0)
         nc.scalar.activation(warm2[:], warm[:], GELU)
 
-        def load_scale_rows(tile, first, rows, queues=(nc.sync,) * 4):
+        def load_scale_rows(tile, first, rows):
             for q in range(4):
-                queues[q].dma_start(
+                nc.sync.dma_start(
                     tile[32 * q + first : 32 * q + first + 4, :].bitcast(I32), rows[4 * q : 4 * q + 4, :].bitcast(I32)
                 )
 
         tab_w = kept([P, T], U32, "tab_w")
         wu_raw = kept([P, 2 * R], U8, "wu_raw")
-        wd8_raw = kept([P, N], I32, "wd8_raw")
-        wd4_raw = kept([P, 2 * N], U8, "wd4_raw")
+        wd8_raw = laid([P, N], I32, "wd8_raw", 1536)
+        wd4_raw = laid([P, 2 * N], U8, "wd4_raw", 0)
         sm_sb = kept([P, 2, 4], F32, "sm_sb")
         wgo_sb = kept([P, J], F32, "wgo_sb")
         nc.sync.dma_start(offsets[:], offs)
+        nc.sync.dma_start(sm_sb[:], sm.rearrange("(a p t) -> p a t", a=2, t=4))
         nc.sync.dma_start(wu_raw[:].bitcast(I32), wu_words[0].bitcast(I32))
+        load_scale_rows(wu_sc_raw, 0, wu_scales[0])
         nc.sync.dma_start(tab_w[:].bitcast(I32), tab_words[0].rearrange("p t i -> p (t i)").bitcast(I32))
         load_scale_rows(tab_sc, 0, tab_scales[0])
-        load_scale_rows(wu_sc_raw, 0, wu_scales[0], (nc.sync, nc.sync, nc.sync, nc.gpsimd))
-        nc.gpsimd.dma_start(sm_sb[:], sm.rearrange("(a p t) -> p a t", a=2, t=4))
         nc.sync.dma_start(wd8_raw[:], wd8_words[0].rearrange("p n i -> p (n i)").bitcast(I32))
         nc.sync.dma_start(wd4_raw[:].bitcast(I32), wd4_words[0].bitcast(I32))
         load_scale_rows(wd_sc_raw, 0, wd4_scales[0])
@@ -94,7 +100,7 @@ def tile_list_modp_gelu_mix_resP_kernel(
 
         def gather_table(c, tag_w=None, tag_sc=None):
             got_sc[c] = kept([P, CH], U8, "got_sc%d" % c, tag_sc)
-            got_w[c] = kept([P, CH], U32, "got_w%d" % c, tag_w)
+            got_w[c] = laid([P, CH], U32, "got_w3", 0) if c == 3 else kept([P, CH], U32, "got_w%d" % c, tag_w)
             nc.vector.tensor_copy(got_sc[c][:], tab_sc[:].indirect(picks(c)))
             nc.vector.tensor_copy(got_w[c][:], tab_w[:].indirect(picks(c)))
 
@@ -113,26 +119,32 @@ def tile_list_modp_gelu_mix_resP_kernel(
 
         h_in = [None] * NCH
 
-        def hidden_first():
-            h_in[0] = kept([P, 2, 2, P, 4], BF16, "h_in0")
+        h_in[0] = [None, None]
+        acts = {}
+
+        def act_first():
             for half in range(2):
                 for a in range(2):
                     cols = slice(P * half, P * (half + 1))
-                    bank = ps_up.tile([P, 4, P], F32, name="up_bank", tag="up")
+                    bank = bank_tile([P, 4, P], 2 * half + a)
                     for t in range(4):
                         up_matmul(bank[:, t, :], 0, a, t, cols)
                     act = kept([P, P, 4], F32, "act_first%d%d" % (a, half))
                     nc.scalar.activation(act[:], bank[:].rearrange("p t j -> p j t"), GELU)
-                    nc.vector.tensor_tensor(
-                        h_in[0][:, half, a], act[:], sm_sb[:, a, :].unsqueeze(1).to_broadcast([P, P, 4]), MULT
-                    )
+                    acts[half, a] = act
+
+        def smooth_first(half):
+            for a in range(2):
+                nc.vector.tensor_tensor(
+                    h_in[0][half][:, a], acts[half, a][:], sm_sb[:, a, :].unsqueeze(1).to_broadcast([P, P, 4]), MULT
+                )
 
         def hidden(c):
             h_in[c] = kept([P, 2, CH, 4], BF16, "h_in%d" % c)
             for a in range(2):
                 flat = ring.tile([P, 4, CH], BF16, name="flat", tag="flat")
                 for u in range(2):
-                    bank = ps_up.tile([P, 2, CH], F32, name="up_bank", tag="up")
+                    bank = bank_tile([P, 2, CH], ((6, 4, 5, 3) if c == 1 else (0, 1, 2, 3))[2 * a + u])
                     for e in range(2):
                         up_matmul(bank[:, e, :], c, a, 2 * u + e, slice(0, CH))
                     act = ring.tile([P, 2, CH], F32, name="act", tag="act")
@@ -144,9 +156,6 @@ def tile_list_modp_gelu_mix_resP_kernel(
                     h_in[c][:, a].rearrange("p (c i) t -> p c t i", i=4), flat[:].rearrange("p t (c i) -> p c t i", i=4)
                 )
 
-        wd8 = kept([P, N], I32, "wd8")
-        wd4 = kept([P, 2 * N], U8, "wd4")
-        wd_sc = kept([P, N], U8, "wd_sc")
         y = [None] * NCH
 
         def down(c):
@@ -159,7 +168,7 @@ def tile_list_modp_gelu_mix_resP_kernel(
             )
             y[c] = [None] * 2
             for u in range(2):
-                bank = ps_down.tile([P, 2, CH], F32, name="down_bank", tag="down")
+                bank = bank_tile([P, 2, CH], 4 + 2 * (c % 2) + u)
                 for e in range(2):
                     t = 2 * u + e
                     for half in range(2):
@@ -178,7 +187,7 @@ def tile_list_modp_gelu_mix_resP_kernel(
                 nc.scalar.copy(y[c][u][:], bank[:])
 
         def down_first():
-            banks = [ps_down.tile([P, 2, CH], F32, name="down_bank", tag="down") for u in range(2)]
+            banks = [bank_tile([P, 2, CH], 4 + u) for u in range(2)]
             y[0] = [kept([P, 2, CH], F32, "y0%d" % u) for u in range(2)]
             for half in range(2):
                 cols = slice(P * half, P * (half + 1))
@@ -187,7 +196,7 @@ def tile_list_modp_gelu_mix_resP_kernel(
                 nc.vector.quantize_mx(
                     out=h_w[:].rearrange("p a j -> p (a j)").bitcast(E4M3),
                     scales=h_sc[:].rearrange("p a j -> p (a j)"),
-                    in_=h_in[0][:, half].rearrange("p a j t -> p (a j t)"),
+                    in_=h_in[0][half][:].rearrange("p a j t -> p (a j t)"),
                 )
                 for t in range(4):
                     out = banks[t // 2][:, t % 2, cols]
@@ -207,25 +216,32 @@ def tile_list_modp_gelu_mix_resP_kernel(
             nc.vector.tensor_tensor(pages[t][:].indirect(picks(c)), total, wgo_sb[:, c * CH : (c + 1) * CH], MULT)
 
         def fresh_total():
-            total = ring.tile([P, CH], F32, name="total", tag="total")
+            total = ring.tile([P, CH], F32, name="total", tag="total", bufs=3)
             return total[:]
 
-        gather_table(0)
         deal_wu(0)
         deal_wu(1)
-        hidden_first()
+        gather_table(0)
+        act_first()
+        h_in[0][0] = kept([P, 2, P, 4], BF16, "h_first0")
+        smooth_first(0)
+        gather_table(1, "wu_raw", "wu_sc_raw")
+        wd8 = kept([P, N], I32, "wd8", "act_first00")
+        wd4 = kept([P, 2 * N], U8, "wd4", "act_first10")
+        wd_sc = kept([P, N], U8, "wd_sc", "got_w0")
         deal(wd8[:], wd8_raw[:])
         deal(wd4[:].bitcast(U16), wd4_raw[:].bitcast(U16))
         deal(wd_sc[:], wd_sc_raw[:])
-        gather_table(1)
+        h_in[0][1] = laid([P, 2, P, 4], BF16, "h_first1", 0)
+        smooth_first(1)
         down_first()
         gather_table(2, "act_first11", "act_first01")
-        gather_table(3, "act_first10", "act_first00")
+        gather_table(3, None, "h_first0")
         for t in range(3):
             pages[t] = kept([P, T], F32, "page%d" % t)
             for half in range(2):
-                nc.vector.memset(pages[t][:, half * T // 2 : (half + 1) * T // 2], 0.0)
-        pages[3] = kept([P, T], F32, "page3", "h_in0")
+                nc.vector.memset(pages[t][:, half * T // 2 : (half + 1) * T // 2].bitcast(I32), 0)
+        pages[3] = kept([P, T], F32, "page3", "tab_w")
         nc.gpsimd.memset(pages[3][:], 0.0)
 
         out_by_plane = out_0.rearrange("(p t) c -> p t c", t=4)

@@ -52,7 +52,7 @@ def tile_list_modp_gelu_mix_resP_kernel(
 
         tab_sc = kept([P, T], U8, "tab_sc")
         wu_sc_raw = kept([P, R], U8, "wu_sc_raw")
-        wd_sc_raw = laid([P, N], U8, "wd_sc_raw", 1024)
+        wd_sc_raw = laid([P, N], U8, "wd_sc_raw", 9216 + 1024)
         nc.vector.memset(wu_sc_raw[:].bitcast(I32), 0)
         nc.vector.memset(tab_sc[:].bitcast(I32), 0)
         nc.vector.memset(wd_sc_raw[:].bitcast(I32), 0)
@@ -70,9 +70,9 @@ def tile_list_modp_gelu_mix_resP_kernel(
                 )
 
         tab_w = kept([P, T], U32, "tab_w")
-        wu_raw = kept([P, 2 * R], U8, "wu_raw")
-        wd8_raw = laid([P, N], I32, "wd8_raw", 1536)
-        wd4_raw = laid([P, 2 * N], U8, "wd4_raw", 0)
+        wu_raw = laid([P, 2 * R], U8, "wu_raw", 0)
+        wd8_raw = laid([P, N], I32, "wd8_raw", 9216 + 1536)
+        wd4_raw = laid([P, 2 * N], U8, "wd4_raw", 9216)
         sm_sb = kept([P, 2, 4], F32, "sm_sb")
         wgo_sb = kept([P, J], F32, "wgo_sb")
         nc.sync.dma_start(offsets[:], offs)
@@ -100,7 +100,7 @@ def tile_list_modp_gelu_mix_resP_kernel(
 
         def gather_table(c, tag_w=None, tag_sc=None):
             got_sc[c] = kept([P, CH], U8, "got_sc%d" % c, tag_sc)
-            got_w[c] = laid([P, CH], U32, "got_w3", 0) if c == 3 else kept([P, CH], U32, "got_w%d" % c, tag_w)
+            got_w[c] = laid([P, CH], U32, "got_w%d" % c, tag_w) if c % 2 else kept([P, CH], U32, "got_w%d" % c, tag_w)
             nc.vector.tensor_copy(got_sc[c][:], tab_sc[:].indirect(picks(c)))
             nc.vector.tensor_copy(got_w[c][:], tab_w[:].indirect(picks(c)))
 
@@ -225,22 +225,24 @@ def tile_list_modp_gelu_mix_resP_kernel(
         act_first()
         h_in[0][0] = kept([P, 2, P, 4], BF16, "h_first0")
         smooth_first(0)
-        gather_table(1, "wu_raw", "wu_sc_raw")
+        gather_table(1, 0, "wu_sc_raw")
+        pages[1] = laid([P, T], F32, "page1", 1024)
+        nc.gpsimd.memset(pages[1][:], 0.0)
         wd8 = kept([P, N], I32, "wd8", "act_first00")
         wd4 = kept([P, 2 * N], U8, "wd4", "act_first10")
         wd_sc = kept([P, N], U8, "wd_sc", "got_w0")
         deal(wd8[:], wd8_raw[:])
         deal(wd4[:].bitcast(U16), wd4_raw[:].bitcast(U16))
         deal(wd_sc[:], wd_sc_raw[:])
-        h_in[0][1] = laid([P, 2, P, 4], BF16, "h_first1", 0)
+        h_in[0][1] = laid([P, 2, P, 4], BF16, "h_first1", 9216)
         smooth_first(1)
         down_first()
         gather_table(2, "act_first11", "act_first01")
-        gather_table(3, None, "h_first0")
-        for t in range(3):
-            pages[t] = kept([P, T], F32, "page%d" % t)
-            for half in range(2):
-                nc.vector.memset(pages[t][:, half * T // 2 : (half + 1) * T // 2].bitcast(I32), 0)
+        gather_table(3, 9216, "h_first0")
+        pages[0] = kept([P, T], F32, "page0")
+        nc.vector.memset(pages[0][:], 0.0)
+        pages[2] = laid([P, T], F32, "page2", 9216 + 1024)
+        nc.gpsimd.memset(pages[2][:], 0.0)
         pages[3] = kept([P, T], F32, "page3", "tab_w")
         nc.gpsimd.memset(pages[3][:], 0.0)
 

@@ -21,7 +21,6 @@ ADD = mybir.AluOpType.add
 P = 128
 CH = 256
 NCH = J // CH
-TAIL = (("v", 256), ("s", 256), ("v", 512), ("s", 512), ("v", 256), ("s", 256))
 
 
 def tile_list_modp_gelu_mix_resP_kernel(
@@ -52,7 +51,7 @@ def tile_list_modp_gelu_mix_resP_kernel(
 
         tab_sc = kept([P, T], U8, "tab_sc")
         wu_sc_raw = kept([P, R], U8, "wu_sc_raw")
-        wd_sc_raw = laid([P, N], U8, "wd_sc_raw", 9216 + 1024)
+        wd_sc_raw = laid([P, N], U8, "wd_sc_raw", 9216)
         nc.vector.memset(wu_sc_raw[:].bitcast(I32), 0)
         nc.vector.memset(tab_sc[:].bitcast(I32), 0)
         nc.vector.memset(wd_sc_raw[:].bitcast(I32), 0)
@@ -71,8 +70,8 @@ def tile_list_modp_gelu_mix_resP_kernel(
 
         tab_w = kept([P, T], U32, "tab_w")
         wu_raw = laid([P, 2 * R], U8, "wu_raw", 0)
-        wd8_raw = laid([P, N], I32, "wd8_raw", 9216 + 1536)
-        wd4_raw = laid([P, 2 * N], U8, "wd4_raw", 9216)
+        wd8_raw = laid([P, N], I32, "wd8_raw", 18432 + 1024)
+        wd4_raw = laid([P, 2 * N], U8, "wd4_raw", 18432)
         sm_sb = kept([P, 2, 4], F32, "sm_sb")
         wgo_sb = kept([P, J], F32, "wgo_sb")
         nc.sync.dma_start(offsets[:], offs)
@@ -99,7 +98,7 @@ def tile_list_modp_gelu_mix_resP_kernel(
         got_sc = [None] * NCH
 
         def gather_table(c, tag_w=None, tag_sc=None):
-            got_sc[c] = kept([P, CH], U8, "got_sc%d" % c, tag_sc)
+            got_sc[c] = laid([P, CH], U8, "got_sc3", 18432) if c == 3 else kept([P, CH], U8, "got_sc%d" % c, tag_sc)
             got_w[c] = laid([P, CH], U32, "got_w%d" % c, tag_w) if c % 2 else kept([P, CH], U32, "got_w%d" % c, tag_w)
             nc.vector.tensor_copy(got_sc[c][:], tab_sc[:].indirect(picks(c)))
             nc.vector.tensor_copy(got_w[c][:], tab_w[:].indirect(picks(c)))
@@ -139,22 +138,31 @@ def tile_list_modp_gelu_mix_resP_kernel(
                     h_in[0][half][:, a], acts[half, a][:], sm_sb[:, a, :].unsqueeze(1).to_broadcast([P, P, 4]), MULT
                 )
 
-        def hidden(c):
-            h_in[c] = kept([P, 2, CH, 4], BF16, "h_in%d" % c)
-            for a in range(2):
-                flat = ring.tile([P, 4, CH], BF16, name="flat", tag="flat")
-                for u in range(2):
-                    bank = bank_tile([P, 2, CH], ((6, 4, 5, 3) if c == 1 else (0, 1, 2, 3))[2 * a + u])
-                    for e in range(2):
-                        up_matmul(bank[:, e, :], c, a, 2 * u + e, slice(0, CH))
-                    act = ring.tile([P, 2, CH], F32, name="act", tag="act")
-                    nc.scalar.activation(act[:], bank[:], GELU)
-                    for e in range(2):
-                        t = 2 * u + e
-                        nc.scalar.activation(flat[:, t, :], act[:, e, :], COPY, scale=sm_sb[:, a, t : t + 1])
-                nc.scalar.copy(
-                    h_in[c][:, a].rearrange("p (c i) t -> p c t i", i=4), flat[:].rearrange("p t (c i) -> p c t i", i=4)
-                )
+        def hidden_half(c, a):
+            if a == 0:
+                h_in[c] = kept([P, 2, CH, 4], BF16, "h_in%d" % c)
+            flat = kept([P, 4, CH], BF16, "flat%d%d" % (c, a))
+            for u in range(2):
+                bank = bank_tile([P, 2, CH], (2 * (c % 2) if a == 0 else 4 + 2 * ((c - 1) % 2)) + u)
+                for e in range(2):
+                    up_matmul(bank[:, e, :], c, a, 2 * u + e, slice(0, CH))
+                act = ring.tile([P, 2, CH], F32, name="act", tag="act")
+                nc.scalar.activation(act[:], bank[:], GELU)
+                for e in range(2):
+                    t = 2 * u + e
+                    nc.scalar.activation(flat[:, t, :], act[:, e, :], COPY, scale=sm_sb[:, a, t : t + 1])
+            nc.scalar.copy(
+                h_in[c][:, a].rearrange("p (c i) t -> p c t i", i=4), flat[:].rearrange("p t (c i) -> p c t i", i=4)
+            )
+
+        def empty_down(c, banks):
+            if c + 1 < NCH:
+                hidden_half(c + 1, 0)
+            y[c] = [kept([P, 2, CH], F32, "y%d0" % c, "flat%d0" % (c + 1)), kept([P, 2, CH], F32, "y%d1" % c)]
+            for u in range(2):
+                nc.scalar.copy(y[c][u][:], banks[u][:])
+            if c + 1 < NCH:
+                hidden_half(c + 1, 1)
 
         y = [None] * NCH
 
@@ -166,9 +174,9 @@ def tile_list_modp_gelu_mix_resP_kernel(
                 scales=h_sc[:].rearrange("p a j -> p (a j)"),
                 in_=h_in[c][:].rearrange("p a j t -> p (a j t)"),
             )
-            y[c] = [None] * 2
+            banks = [bank_tile([P, 2, CH], 4 + 2 * (c % 2) + u) for u in range(2)]
             for u in range(2):
-                bank = bank_tile([P, 2, CH], 4 + 2 * (c % 2) + u)
+                bank = banks[u]
                 for e in range(2):
                     t = 2 * u + e
                     for half in range(2):
@@ -183,12 +191,10 @@ def tile_list_modp_gelu_mix_resP_kernel(
                             lhsT_scale=wd_sc[:, P * t : P * (t + 1)],
                             rhs=h_w[:, 1, cols].bitcast(E4M3), rhs_scale=h_sc[:, 1, cols], start=False, stop=True,
                         )
-                y[c][u] = kept([P, 2, CH], F32, "y%d%d" % (c, u))
-                nc.scalar.copy(y[c][u][:], bank[:])
+            empty_down(c, banks)
 
         def down_first():
             banks = [bank_tile([P, 2, CH], 4 + u) for u in range(2)]
-            y[0] = [kept([P, 2, CH], F32, "y0%d" % u) for u in range(2)]
             for half in range(2):
                 cols = slice(P * half, P * (half + 1))
                 h_w = kept([P, 2, P], U32, "h_w_first%d" % half)
@@ -208,37 +214,43 @@ def tile_list_modp_gelu_mix_resP_kernel(
                         out, lhsT=wd4[:, 256 * t : 256 * (t + 1)].bitcast(E2M1), lhsT_scale=wd_sc[:, P * t : P * (t + 1)],
                         rhs=h_w[:, 1, :].bitcast(E4M3), rhs_scale=h_sc[:, 1, :], start=False, stop=True,
                     )
-                    if half == 1 and t % 2 == 1:
-                        nc.scalar.copy(y[0][t // 2][:], banks[t // 2][:])
+            empty_down(0, banks)
 
-        def place(c, t, total):
-            nc.vector.tensor_tensor(total, res[t][:].indirect(picks(c)), y[c][t // 2][:, t % 2, :], ADD)
-            nc.vector.tensor_tensor(pages[t][:].indirect(picks(c)), total, wgo_sb[:, c * CH : (c + 1) * CH], MULT)
+        def place_pair(c, u, totals, after):
+            for e in range(2):
+                nc.vector.tensor_tensor(totals[:, e, :], res[2 * u + e][:].indirect(picks(c)), y[c][u][:, e, :], ADD)
+            for e in range(2):
+                t = 2 * u + e
+                nc.vector.tensor_tensor(
+                    pages[t][:].indirect(picks(c)), totals[:, e, :], wgo_sb[:, c * CH : (c + 1) * CH], MULT
+                )
+                if after:
+                    after(t)
 
-        def fresh_total():
-            total = ring.tile([P, CH], F32, name="total", tag="total", bufs=3)
-            return total[:]
+        def fresh_totals():
+            totals = ring.tile([P, 2, CH], F32, name="totals", tag="totals")
+            return totals[:]
 
         deal_wu(0)
         deal_wu(1)
         gather_table(0)
         act_first()
-        h_in[0][0] = kept([P, 2, P, 4], BF16, "h_first0")
-        smooth_first(0)
         gather_table(1, 0, "wu_sc_raw")
         pages[1] = laid([P, T], F32, "page1", 1024)
         nc.gpsimd.memset(pages[1][:], 0.0)
-        wd8 = kept([P, N], I32, "wd8", "act_first00")
-        wd4 = kept([P, 2 * N], U8, "wd4", "act_first10")
+        wd8 = kept([P, N], I32, "wd8")
+        wd4 = kept([P, 2 * N], U8, "wd4")
         wd_sc = kept([P, N], U8, "wd_sc", "got_w0")
         deal(wd8[:], wd8_raw[:])
         deal(wd4[:].bitcast(U16), wd4_raw[:].bitcast(U16))
+        h_in[0][0] = laid([P, 2, P, 4], BF16, "h_first0", 18432)
+        smooth_first(0)
         deal(wd_sc[:], wd_sc_raw[:])
         h_in[0][1] = laid([P, 2, P, 4], BF16, "h_first1", 9216)
         smooth_first(1)
         down_first()
         gather_table(2, "act_first11", "act_first01")
-        gather_table(3, 9216, "h_first0")
+        gather_table(3, 9216)
         pages[0] = kept([P, T], F32, "page0")
         nc.vector.memset(pages[0][:], 0.0)
         pages[2] = laid([P, T], F32, "page2", 9216 + 1024)
@@ -247,42 +259,63 @@ def tile_list_modp_gelu_mix_resP_kernel(
         nc.gpsimd.memset(pages[3][:], 0.0)
 
         out_by_plane = out_0.rearrange("(p t) c -> p t c", t=4)
-        starts = [sum(w for e, w in TAIL[:k]) for k in range(len(TAIL))]
-        flat_out = [kept([P, 4, w], BF16, "flat_out%d" % k) for k, (e, w) in enumerate(TAIL)]
+        HALF = T // 2
+        flat_out = [kept([P, 4, HALF], BF16, "flat_out%d" % k) for k in range(2)]
 
         def finish_plane(t):
             nc.sync.dma_start(out_by_plane[:, t, :], pages[t][:])
             if t < 3:
-                for k, (e, w) in enumerate(TAIL):
-                    nc.scalar.copy(flat_out[k][:, t, :], pages[t][:, starts[k] : starts[k] + w])
+                for k in range(2):
+                    nc.scalar.copy(flat_out[k][:, t, :], pages[t][:, k * HALF : (k + 1) * HALF])
 
         for c in range(NCH):
             last = c == NCH - 1
-            if not last:
-                hidden(c + 1)
-            for t in range(3):
-                place(c, t, fresh_total())
-                if last:
-                    finish_plane(t)
+            place_pair(c, 0, fresh_totals(), finish_plane if last else None)
             if last:
-                place(c, 3, fresh_total())
-                finish_plane(3)
+                place_pair(c, 1, fresh_totals(), finish_plane)
             else:
                 down(c + 1)
-                place(c, 3, h_in[c + 1][:].rearrange("p a j t -> p (a j t)").bitcast(F32)[:, 0:CH])
+                spent = h_in[c + 1][:, 0].rearrange("p j t -> p (j t)").bitcast(F32)
+                place_pair(c, 1, spent.rearrange("p (e j) -> p e j", e=2), None)
 
         out_w = kept([P, T], U32, "out_w")
         out_sc = kept([P, T], U8, "out_sc")
         out_words = out_1[0].rearrange("p t i -> p (t i)").bitcast(I32)
-        for k, (e, w) in enumerate(TAIL):
-            cols = slice(starts[k], starts[k] + w)
-            copy = nc.vector.tensor_copy if e == "v" else nc.scalar.copy
-            woven = kept([P, w, 4], BF16, "woven%d" % k)
-            copy(flat_out[k][:, 3, :], pages[3][:, cols])
-            copy(woven[:].rearrange("p (c i) t -> p c t i", i=4), flat_out[k][:].rearrange("p t (c i) -> p c t i", i=4))
+        copies = (nc.vector.tensor_copy, nc.scalar.copy)
+        pieces = ((0, 256), (256, 768), (768, 1024))
+        woven = {}
+
+        def round_last(k, lo, hi):
+            copies[k](flat_out[k][:, 3, lo:hi], pages[3][:, k * HALF + lo : k * HALF + hi])
+
+        def weave(k, n):
+            lo, hi = pieces[n]
+            woven[k, n] = kept([P, hi - lo, 4], BF16, "woven%d%d" % (k, n))
+            copies[k](
+                woven[k, n][:].rearrange("p (c i) t -> p c t i", i=4),
+                flat_out[k][:, :, lo:hi].rearrange("p t (c i) -> p c t i", i=4),
+            )
+
+        def quantize_out(k, n):
+            cols = slice(k * HALF + pieces[n][0], k * HALF + pieces[n][1])
             nc.vector.quantize_mx(
-                out=out_w[:, cols].bitcast(E4M3), scales=out_sc[:, cols], in_=woven[:].rearrange("p c t -> p (c t)")
+                out=out_w[:, cols].bitcast(E4M3), scales=out_sc[:, cols], in_=woven[k, n][:].rearrange("p c t -> p (c t)")
             )
             nc.sync.dma_start(out_words[:, cols], out_w[:, cols].bitcast(I32))
+
+        for k in range(2):
+            round_last(k, 0, 256)
+            round_last(k, 256, HALF)
+        for n in range(3):
+            weave(1, n)
+        weave(0, 0)
+        weave(0, 1)
+        quantize_out(0, 0)
+        quantize_out(1, 0)
+        quantize_out(0, 1)
+        weave(0, 2)
+        quantize_out(1, 1)
+        quantize_out(0, 2)
+        quantize_out(1, 2)
         for q in range(4):
             nc.scalar.dma_start(out_2[0, 4 * q : 4 * q + 4, :].bitcast(I32), out_sc[32 * q : 32 * q + 4, :].bitcast(I32))

@@ -19,8 +19,14 @@ MULT = mybir.AluOpType.mult
 ADD = mybir.AluOpType.add
 
 P = 128
+PASS = 512
 CH = 256
 NCH = J // CH
+LAST = NCH - 1
+WD8_ROW = 4
+KIB = 1024
+AREA_A, AREA_B, AREA_C = 0, 9 * KIB, 18 * KIB
+SPLIT = 1408
 
 
 def tile_list_modp_gelu_mix_resP_kernel(
@@ -32,17 +38,17 @@ def tile_list_modp_gelu_mix_resP_kernel(
         lists = ctx.enter_context(tc.tile_pool(name="lists", bufs=1))
         keep = ctx.enter_context(tc.tile_pool(name="keep", bufs=1))
         ring = ctx.enter_context(tc.tile_pool(name="ring", bufs=2))
-        shared = ctx.enter_context(tc.tile_pool(name="shared", bufs=1))
+        placed = ctx.enter_context(tc.tile_pool(name="placed", bufs=1))
         psum = ctx.enter_context(tc.psum_pool(name="psum", bufs=1))
+
+        def kept(shape, dtype, name, on=None):
+            return keep.tile(shape, dtype, name=name, tag=on or name, align_bytes=64)
+
+        def laid(shape, dtype, name, offset):
+            return placed.tile(shape, dtype, name=name, tag=name, align_bytes=64, offset=offset)
 
         def bank_tile(shape, b):
             return psum.tile(shape, F32, name="bank%d" % b, tag="bank%d" % b)
-
-        def kept(shape, dtype, name, tag=None):
-            return keep.tile(shape, dtype, name=name, tag=tag or name, align_bytes=64)
-
-        def laid(shape, dtype, name, offset):
-            return shared.tile(shape, dtype, name=name, tag=name, align_bytes=64, offset=offset)
 
         offsets = lists.tile([P, J // 16], U16, name="offsets")
 
@@ -51,16 +57,10 @@ def tile_list_modp_gelu_mix_resP_kernel(
 
         tab_sc = kept([P, T], U8, "tab_sc")
         wu_sc_raw = kept([P, R], U8, "wu_sc_raw")
-        wd_sc_raw = laid([P, N], U8, "wd_sc_raw", 9216)
+        wd_sc_raw = laid([P, N], U8, "wd_sc_raw", AREA_B)
         nc.vector.memset(wu_sc_raw[:].bitcast(I32), 0)
         nc.vector.memset(tab_sc[:].bitcast(I32), 0)
         nc.vector.memset(wd_sc_raw[:].bitcast(I32), 0)
-        pages = [None] * 4
-
-        warm = kept([P, 1], F32, "warm")
-        warm2 = kept([P, 1], F32, "warm2")
-        nc.gpsimd.memset(warm[:], 0.0)
-        nc.scalar.activation(warm2[:], warm[:], GELU)
 
         def load_scale_rows(tile, first, rows):
             for q in range(4):
@@ -69,11 +69,13 @@ def tile_list_modp_gelu_mix_resP_kernel(
                 )
 
         tab_w = kept([P, T], U32, "tab_w")
-        wu_raw = laid([P, 2 * R], U8, "wu_raw", 0)
-        wd8_raw = laid([P, N], I32, "wd8_raw", 18432 + 1024)
-        wd4_raw = laid([P, 2 * N], U8, "wd4_raw", 18432)
+        wu_raw = laid([P, 2 * R], U8, "wu_raw", AREA_A)
+        wd8_raw = laid([P, N], I32, "wd8_raw", AREA_C + KIB)
+        wd4_raw = laid([P, 2 * N], U8, "wd4_raw", AREA_C)
         sm_sb = kept([P, 2, 4], F32, "sm_sb")
         wgo_sb = kept([P, J], F32, "wgo_sb")
+        res = [kept([P, T], F32, "res%d" % t) for t in range(4)]
+        rT_planes = rT.rearrange("(p t) c -> p t c", t=4)
         nc.sync.dma_start(offsets[:], offs)
         nc.sync.dma_start(sm_sb[:], sm.rearrange("(a p t) -> p a t", a=2, t=4))
         nc.sync.dma_start(wu_raw[:].bitcast(I32), wu_words[0].bitcast(I32))
@@ -83,239 +85,248 @@ def tile_list_modp_gelu_mix_resP_kernel(
         nc.sync.dma_start(wd8_raw[:], wd8_words[0].rearrange("p n i -> p (n i)").bitcast(I32))
         nc.sync.dma_start(wd4_raw[:].bitcast(I32), wd4_words[0].bitcast(I32))
         load_scale_rows(wd_sc_raw, 0, wd4_scales[0])
-        load_scale_rows(wd_sc_raw, 4, wd8_scales[0])
-        res = [kept([P, T], F32, "res%d" % t) for t in range(4)]
-        rT_by_plane = rT.rearrange("(p t) c -> p t c", t=4)
-        nc.sync.dma_start(res[0][:], rT_by_plane[:, 0, :])
+        load_scale_rows(wd_sc_raw, WD8_ROW, wd8_scales[0])
+        nc.sync.dma_start(res[0][:], rT_planes[:, 0, :])
         nc.sync.dma_start(wgo_sb[:], wgo)
         for t in range(1, 4):
-            nc.sync.dma_start(res[t][:], rT_by_plane[:, t, :])
+            nc.sync.dma_start(res[t][:], rT_planes[:, t, :])
 
         def deal(dst, src):
             nc.vector.tensor_copy(dst.rearrange("p (t m) -> p t m", t=4), src.rearrange("p (m t) -> p t m", t=4))
 
-        got_w = [None] * NCH
-        got_sc = [None] * NCH
+        def weave_on_scalar(dst, planes):
+            nc.scalar.copy(dst.rearrange("p (c i) t -> p c t i", i=4), planes.rearrange("p t (c i) -> p c t i", i=4))
 
-        def gather_table(c, tag_w=None, tag_sc=None):
-            got_sc[c] = laid([P, CH], U8, "got_sc3", 18432) if c == 3 else kept([P, CH], U8, "got_sc%d" % c, tag_sc)
-            got_w[c] = laid([P, CH], U32, "got_w%d" % c, tag_w) if c % 2 else kept([P, CH], U32, "got_w%d" % c, tag_w)
-            nc.vector.tensor_copy(got_sc[c][:], tab_sc[:].indirect(picks(c)))
-            nc.vector.tensor_copy(got_w[c][:], tab_w[:].indirect(picks(c)))
+        got_w = {}
+        got_sc = {}
 
-        wu = [kept([P, 1024], U8, "wu%d" % a) for a in range(2)]
-        wu_sc = [kept([P, 512], U8, "wu_sc%d" % a) for a in range(2)]
+        def gather_table(c, words, scales):
+            got_w[c], got_sc[c] = words, scales
+            nc.vector.tensor_copy(scales[:], tab_sc[:].indirect(picks(c)))
+            nc.vector.tensor_copy(words[:], tab_w[:].indirect(picks(c)))
 
-        def deal_wu(a):
-            deal(wu[a][:].bitcast(U16), wu_raw[:].bitcast(U16)[:, 512 * a : 512 * (a + 1)])
-            deal(wu_sc[a][:], wu_sc_raw[:, 512 * a : 512 * (a + 1)])
+        wu = [kept([P, 2 * PASS], U8, "wu%d" % a) for a in range(2)]
+        wu_sc = [kept([P, PASS], U8, "wu_sc%d" % a) for a in range(2)]
 
         def up_matmul(out, c, a, t, cols):
             nc.tensor.matmul_mx(
-                out, lhsT=wu[a][:, 256 * t : 256 * (t + 1)].bitcast(E2M1), lhsT_scale=wu_sc[a][:, P * t : P * (t + 1)],
+                out, lhsT=wu[a][:, 2 * P * t : 2 * P * (t + 1)].bitcast(E2M1),
+                lhsT_scale=wu_sc[a][:, P * t : P * (t + 1)],
                 rhs=got_w[c][:, cols].bitcast(E4M3), rhs_scale=got_sc[c][:, cols], start=True, stop=True,
             )
 
-        h_in = [None] * NCH
+        def down_matmuls(out, t, words, scales):
+            nc.tensor.matmul_mx(
+                out, lhsT=wd8[:, P * t : P * (t + 1)].bitcast(E4M3), lhsT_scale=wd_sc[WD8_ROW:P, P * t : P * (t + 1)],
+                rhs=words[0].bitcast(E4M3), rhs_scale=scales[0], start=True, stop=False,
+            )
+            nc.tensor.matmul_mx(
+                out, lhsT=wd4[:, 2 * P * t : 2 * P * (t + 1)].bitcast(E2M1), lhsT_scale=wd_sc[:, P * t : P * (t + 1)],
+                rhs=words[1].bitcast(E4M3), rhs_scale=scales[1], start=False, stop=True,
+            )
 
-        h_in[0] = [None, None]
-        acts = {}
+        def quantize_h(words, scales, woven_h):
+            nc.vector.quantize_mx(
+                out=words.rearrange("p a j -> p (a j)").bitcast(E4M3),
+                scales=scales.rearrange("p a j -> p (a j)"),
+                in_=woven_h.rearrange("p a j t -> p (a j t)"),
+            )
 
-        def act_first():
-            for half in range(2):
-                for a in range(2):
-                    cols = slice(P * half, P * (half + 1))
-                    bank = bank_tile([P, 4, P], 2 * half + a)
-                    for t in range(4):
-                        up_matmul(bank[:, t, :], 0, a, t, cols)
-                    act = kept([P, P, 4], F32, "act_first%d%d" % (a, half))
-                    nc.scalar.activation(act[:], bank[:].rearrange("p t j -> p j t"), GELU)
-                    acts[half, a] = act
+        def down_bank(c, u):
+            return 4 + 2 * (c % 2) + u
 
-        def smooth_first(half):
-            for a in range(2):
-                nc.vector.tensor_tensor(
-                    h_in[0][half][:, a], acts[half, a][:], sm_sb[:, a, :].unsqueeze(1).to_broadcast([P, P, 4]), MULT
-                )
+        h_in = {}
+        y = {}
 
-        def hidden_half(c, a):
+        def hidden_pass(c, a):
             if a == 0:
                 h_in[c] = kept([P, 2, CH, 4], BF16, "h_in%d" % c)
-            flat = kept([P, 4, CH], BF16, "flat%d%d" % (c, a))
+            h_planes = kept([P, 4, CH], BF16, "h_planes%d%d" % (c, a))
             for u in range(2):
-                bank = bank_tile([P, 2, CH], (2 * (c % 2) if a == 0 else 4 + 2 * ((c - 1) % 2)) + u)
+                bank = bank_tile([P, 2, CH], 2 * (c % 2) + u if a == 0 else down_bank(c - 1, u))
                 for e in range(2):
                     up_matmul(bank[:, e, :], c, a, 2 * u + e, slice(0, CH))
                 act = ring.tile([P, 2, CH], F32, name="act", tag="act")
                 nc.scalar.activation(act[:], bank[:], GELU)
                 for e in range(2):
                     t = 2 * u + e
-                    nc.scalar.activation(flat[:, t, :], act[:, e, :], COPY, scale=sm_sb[:, a, t : t + 1])
-            nc.scalar.copy(
-                h_in[c][:, a].rearrange("p (c i) t -> p c t i", i=4), flat[:].rearrange("p t (c i) -> p c t i", i=4)
-            )
+                    nc.scalar.activation(h_planes[:, t, :], act[:, e, :], COPY, scale=sm_sb[:, a, t : t + 1])
+            weave_on_scalar(h_in[c][:, a], h_planes[:])
 
         def empty_down(c, banks):
-            if c + 1 < NCH:
-                hidden_half(c + 1, 0)
-            y[c] = [kept([P, 2, CH], F32, "y%d0" % c, "flat%d0" % (c + 1)), kept([P, 2, CH], F32, "y%d1" % c)]
+            if c < LAST:
+                hidden_pass(c + 1, 0)
+            on = "h_planes%d0" % (c + 1) if c < LAST else None
+            y[c] = [kept([P, 2, CH], F32, "y%d0" % c, on), kept([P, 2, CH], F32, "y%d1" % c)]
             for u in range(2):
                 nc.scalar.copy(y[c][u][:], banks[u][:])
-            if c + 1 < NCH:
-                hidden_half(c + 1, 1)
-
-        y = [None] * NCH
+            if c < LAST:
+                hidden_pass(c + 1, 1)
 
         def down(c):
             h_w = ring.tile([P, 2, CH], U32, name="h_w", tag="h_w", align_bytes=64)
             h_sc = ring.tile([P, 2, CH], U8, name="h_sc", tag="h_sc", align_bytes=64)
-            nc.vector.quantize_mx(
-                out=h_w[:].rearrange("p a j -> p (a j)").bitcast(E4M3),
-                scales=h_sc[:].rearrange("p a j -> p (a j)"),
-                in_=h_in[c][:].rearrange("p a j t -> p (a j t)"),
-            )
-            banks = [bank_tile([P, 2, CH], 4 + 2 * (c % 2) + u) for u in range(2)]
-            for u in range(2):
-                bank = banks[u]
-                for e in range(2):
-                    t = 2 * u + e
-                    for half in range(2):
-                        cols = slice(P * half, P * (half + 1))
-                        nc.tensor.matmul_mx(
-                            bank[:, e, cols], lhsT=wd8[:, P * t : P * (t + 1)].bitcast(E4M3),
-                            lhsT_scale=wd_sc[4:P, P * t : P * (t + 1)],
-                            rhs=h_w[:, 0, cols].bitcast(E4M3), rhs_scale=h_sc[:, 0, cols], start=True, stop=False,
-                        )
-                        nc.tensor.matmul_mx(
-                            bank[:, e, cols], lhsT=wd4[:, 256 * t : 256 * (t + 1)].bitcast(E2M1),
-                            lhsT_scale=wd_sc[:, P * t : P * (t + 1)],
-                            rhs=h_w[:, 1, cols].bitcast(E4M3), rhs_scale=h_sc[:, 1, cols], start=False, stop=True,
-                        )
+            quantize_h(h_w[:], h_sc[:], h_in[c][:])
+            banks = [bank_tile([P, 2, CH], down_bank(c, u)) for u in range(2)]
+            for t in range(4):
+                for half in range(2):
+                    cols = slice(P * half, P * (half + 1))
+                    down_matmuls(
+                        banks[t // 2][:, t % 2, cols], t,
+                        [h_w[:, a, cols] for a in range(2)], [h_sc[:, a, cols] for a in range(2)],
+                    )
             empty_down(c, banks)
 
-        def down_first():
-            banks = [bank_tile([P, 2, CH], 4 + u) for u in range(2)]
-            for half in range(2):
-                cols = slice(P * half, P * (half + 1))
-                h_w = kept([P, 2, P], U32, "h_w_first%d" % half)
-                h_sc = kept([P, 2, P], U8, "h_sc_first%d" % half)
-                nc.vector.quantize_mx(
-                    out=h_w[:].rearrange("p a j -> p (a j)").bitcast(E4M3),
-                    scales=h_sc[:].rearrange("p a j -> p (a j)"),
-                    in_=h_in[0][half][:].rearrange("p a j t -> p (a j t)"),
-                )
+        for a in range(2):
+            deal(wu[a][:].bitcast(U16), wu_raw[:].bitcast(U16)[:, PASS * a : PASS * (a + 1)])
+            deal(wu_sc[a][:], wu_sc_raw[:, PASS * a : PASS * (a + 1)])
+        gather_table(0, kept([P, CH], U32, "got_w0"), kept([P, CH], U8, "got_sc0"))
+        act_first = {}
+        for half in range(2):
+            for a in range(2):
+                bank = bank_tile([P, 4, P], 2 * half + a)
                 for t in range(4):
-                    out = banks[t // 2][:, t % 2, cols]
-                    nc.tensor.matmul_mx(
-                        out, lhsT=wd8[:, P * t : P * (t + 1)].bitcast(E4M3), lhsT_scale=wd_sc[4:P, P * t : P * (t + 1)],
-                        rhs=h_w[:, 0, :].bitcast(E4M3), rhs_scale=h_sc[:, 0, :], start=True, stop=False,
-                    )
-                    nc.tensor.matmul_mx(
-                        out, lhsT=wd4[:, 256 * t : 256 * (t + 1)].bitcast(E2M1), lhsT_scale=wd_sc[:, P * t : P * (t + 1)],
-                        rhs=h_w[:, 1, :].bitcast(E4M3), rhs_scale=h_sc[:, 1, :], start=False, stop=True,
-                    )
-            empty_down(0, banks)
+                    up_matmul(bank[:, t, :], 0, a, t, slice(P * half, P * (half + 1)))
+                act_first[half, a] = kept([P, P, 4], F32, "act_first%d%d" % (half, a))
+                nc.scalar.activation(act_first[half, a][:], bank[:].rearrange("p t j -> p j t"), GELU)
 
-        def place_pair(c, u, totals, after):
-            for e in range(2):
-                nc.vector.tensor_tensor(totals[:, e, :], res[2 * u + e][:].indirect(picks(c)), y[c][u][:, e, :], ADD)
-            for e in range(2):
-                t = 2 * u + e
-                nc.vector.tensor_tensor(
-                    pages[t][:].indirect(picks(c)), totals[:, e, :], wgo_sb[:, c * CH : (c + 1) * CH], MULT
-                )
-                if after:
-                    after(t)
+        def smooth_first(half, woven_h):
+            for a in range(2):
+                factors = sm_sb[:, a, :].unsqueeze(1).to_broadcast([P, P, 4])
+                nc.vector.tensor_tensor(woven_h[:, a], act_first[half, a][:], factors, MULT)
 
-        def fresh_totals():
-            totals = ring.tile([P, 2, CH], F32, name="totals", tag="totals")
-            return totals[:]
-
-        deal_wu(0)
-        deal_wu(1)
-        gather_table(0)
-        act_first()
-        gather_table(1, 0, "wu_sc_raw")
-        pages[1] = laid([P, T], F32, "page1", 1024)
+        pages = {}
+        gather_table(1, laid([P, CH], U32, "got_w1", AREA_A), kept([P, CH], U8, "got_sc1", "wu_sc_raw"))
+        pages[1] = laid([P, T], F32, "page1", AREA_A + KIB)
         nc.gpsimd.memset(pages[1][:], 0.0)
         wd8 = kept([P, N], I32, "wd8")
         wd4 = kept([P, 2 * N], U8, "wd4")
         wd_sc = kept([P, N], U8, "wd_sc", "got_w0")
         deal(wd8[:], wd8_raw[:])
         deal(wd4[:].bitcast(U16), wd4_raw[:].bitcast(U16))
-        h_in[0][0] = laid([P, 2, P, 4], BF16, "h_first0", 18432)
-        smooth_first(0)
+        h_first = [laid([P, 2, P, 4], BF16, "h_first0", AREA_C)]
+        smooth_first(0, h_first[0])
         deal(wd_sc[:], wd_sc_raw[:])
-        h_in[0][1] = laid([P, 2, P, 4], BF16, "h_first1", 9216)
-        smooth_first(1)
-        down_first()
-        gather_table(2, "act_first11", "act_first01")
-        gather_table(3, 9216)
+        h_first.append(laid([P, 2, P, 4], BF16, "h_first1", AREA_B))
+        smooth_first(1, h_first[1])
+        first_banks = [bank_tile([P, 2, CH], down_bank(0, u)) for u in range(2)]
+        for half in range(2):
+            h_w_first = kept([P, 2, P], U32, "h_w_first%d" % half)
+            h_sc_first = kept([P, 2, P], U8, "h_sc_first%d" % half)
+            quantize_h(h_w_first[:], h_sc_first[:], h_first[half][:])
+            for t in range(4):
+                down_matmuls(
+                    first_banks[t // 2][:, t % 2, P * half : P * (half + 1)], t,
+                    [h_w_first[:, a, :] for a in range(2)], [h_sc_first[:, a, :] for a in range(2)],
+                )
+        empty_down(0, first_banks)
+        gather_table(2, kept([P, CH], U32, "got_w2", "act_first11"), kept([P, CH], U8, "got_sc2", "act_first10"))
+        gather_table(3, laid([P, CH], U32, "got_w3", AREA_B), laid([P, CH], U8, "got_sc3", AREA_C))
         pages[0] = kept([P, T], F32, "page0")
         nc.vector.memset(pages[0][:], 0.0)
-        pages[2] = laid([P, T], F32, "page2", 9216 + 1024)
+        pages[2] = laid([P, T], F32, "page2", AREA_B + KIB)
         nc.gpsimd.memset(pages[2][:], 0.0)
         pages[3] = kept([P, T], F32, "page3", "tab_w")
         nc.gpsimd.memset(pages[3][:], 0.0)
 
-        out_by_plane = out_0.rearrange("(p t) c -> p t c", t=4)
-        HALF = T // 2
-        flat_out = [kept([P, 4, HALF], BF16, "flat_out%d" % k) for k in range(2)]
+        def add_residual(c, t, total):
+            nc.vector.tensor_tensor(total, res[t][:].indirect(picks(c)), y[c][t // 2][:, t % 2, :], ADD)
+
+        def scatter(c, t, total):
+            nc.vector.tensor_tensor(pages[t][:].indirect(picks(c)), total, wgo_sb[:, c * CH : (c + 1) * CH], MULT)
+
+        def fresh_totals():
+            totals = ring.tile([P, 2, CH], F32, name="totals", tag="totals")
+            return totals[:]
+
+        out_planes = out_0.rearrange("(p t) c -> p t c", t=4)
+        pairs = kept([P, 2, SPLIT, 2], BF16, "pairs")
+        rounded = kept([P, 4, T - SPLIT], BF16, "rounded")
 
         def finish_plane(t):
-            nc.sync.dma_start(out_by_plane[:, t, :], pages[t][:])
+            nc.sync.dma_start(out_planes[:, t, :], pages[t][:])
+            if t < 2:
+                nc.scalar.copy(pairs[:, 0, :, t], pages[t][:, 0:SPLIT])
+            if t == 2:
+                nc.scalar.copy(pairs[:, 1], pages[t][:, 0:SPLIT].unsqueeze(2).to_broadcast([P, SPLIT, 2]))
             if t < 3:
-                for k in range(2):
-                    nc.scalar.copy(flat_out[k][:, t, :], pages[t][:, k * HALF : (k + 1) * HALF])
+                nc.scalar.copy(rounded[:, t, :], pages[t][:, SPLIT:T])
 
-        for c in range(NCH):
-            last = c == NCH - 1
-            place_pair(c, 0, fresh_totals(), finish_plane if last else None)
-            if last:
-                place_pair(c, 1, fresh_totals(), finish_plane)
-            else:
-                down(c + 1)
-                spent = h_in[c + 1][:, 0].rearrange("p j t -> p (j t)").bitcast(F32)
-                place_pair(c, 1, spent.rearrange("p (e j) -> p e j", e=2), None)
+        for c in range(LAST):
+            totals = fresh_totals()
+            for t in (0, 1):
+                add_residual(c, t, totals[:, t, :])
+            for t in (0, 1):
+                scatter(c, t, totals[:, t, :])
+            down(c + 1)
+            spent = h_in[c + 1][:, 0].rearrange("p j t -> p (j t)").bitcast(F32).rearrange("p (e j) -> p e j", e=2)
+            planes = (2, 3) if c < LAST - 1 else (2,)
+            for t in planes:
+                add_residual(c, t, spent[:, t - 2, :])
+            for t in planes:
+                scatter(c, t, spent[:, t - 2, :])
+        low, high = fresh_totals(), fresh_totals()
+        for t in (0, 1):
+            add_residual(LAST, t, low[:, t, :])
+        for t in (0, 1):
+            scatter(LAST, t, low[:, t, :])
+            finish_plane(t)
+        for t in (2, 3):
+            add_residual(LAST, t, high[:, t - 2, :])
+        scatter(LAST, 2, high[:, 0, :])
+        finish_plane(2)
+        add_residual(LAST - 1, 3, low[:, 1, :])
+        scatter(LAST, 3, high[:, 1, :])
+        scatter(LAST - 1, 3, low[:, 1, :])
+        finish_plane(3)
 
         out_w = kept([P, T], U32, "out_w")
         out_sc = kept([P, T], U8, "out_sc")
         out_words = out_1[0].rearrange("p t i -> p (t i)").bitcast(I32)
-        copies = (nc.vector.tensor_copy, nc.scalar.copy)
-        pieces = ((0, 256), (256, 768), (768, 1024))
+        pair_words = pairs[:].rearrange("p u c e -> p u (c e)").bitcast(F32)
         woven = {}
 
-        def round_last(k, lo, hi):
-            copies[k](flat_out[k][:, 3, lo:hi], pages[3][:, k * HALF + lo : k * HALF + hi])
-
-        def weave(k, n):
-            lo, hi = pieces[n]
-            woven[k, n] = kept([P, hi - lo, 4], BF16, "woven%d%d" % (k, n))
-            copies[k](
-                woven[k, n][:].rearrange("p (c i) t -> p c t i", i=4),
-                flat_out[k][:, :, lo:hi].rearrange("p t (c i) -> p c t i", i=4),
+        def vector_piece(lo, hi):
+            woven[lo] = kept([P, hi - lo, 4], BF16, "woven%d" % lo)
+            nc.vector.tensor_copy(
+                woven[lo][:].rearrange("p c t -> p (c t)").bitcast(F32).rearrange("p (c u) -> p c u", u=2),
+                pair_words[:, :, lo:hi].rearrange("p u c -> p c u"),
             )
 
-        def quantize_out(k, n):
-            cols = slice(k * HALF + pieces[n][0], k * HALF + pieces[n][1])
+        def scalar_piece(lo, hi):
+            woven[lo] = kept([P, hi - lo, 4], BF16, "woven%d" % lo)
+            nc.scalar.copy(rounded[:, 3, lo - SPLIT : hi - SPLIT], pages[3][:, lo:hi])
+            weave_on_scalar(woven[lo][:], rounded[:, :, lo - SPLIT : hi - SPLIT])
+
+        def quantize_out(lo, hi):
             nc.vector.quantize_mx(
-                out=out_w[:, cols].bitcast(E4M3), scales=out_sc[:, cols], in_=woven[k, n][:].rearrange("p c t -> p (c t)")
+                out=out_w[:, lo:hi].bitcast(E4M3), scales=out_sc[:, lo:hi], in_=woven[lo][:].rearrange("p c t -> p (c t)")
             )
-            nc.sync.dma_start(out_words[:, cols], out_w[:, cols].bitcast(I32))
 
-        for k in range(2):
-            round_last(k, 0, 256)
-            round_last(k, 256, HALF)
-        for n in range(3):
-            weave(1, n)
-        weave(0, 0)
-        weave(0, 1)
-        quantize_out(0, 0)
-        quantize_out(1, 0)
-        quantize_out(0, 1)
-        weave(0, 2)
-        quantize_out(1, 1)
-        quantize_out(0, 2)
-        quantize_out(1, 2)
+        def store_codes(lo, hi):
+            nc.sync.dma_start(out_words[:, lo:hi], out_w[:, lo:hi].bitcast(I32))
+
+        v0, v1, v2, v3 = (0, 256), (256, 768), (768, 1280), (1280, SPLIT)
+        s0, s1, s2 = (SPLIT, 1664), (1664, 1920), (1920, T)
+        nc.vector.tensor_copy(pairs[:, 1, v0[0] : v1[1], 1], pages[3][:, v0[0] : v1[1]])
+        nc.vector.tensor_copy(pairs[:, 1, v2[0] : v3[1], 1], pages[3][:, v2[0] : v3[1]])
+        for piece in (s0, s1, s2):
+            scalar_piece(*piece)
+        vector_piece(*v0)
+        vector_piece(*v1)
+        quantize_out(*v0)
+        vector_piece(*v2)
+        quantize_out(*v1)
+        store_codes(v0[0], v1[1])
+        vector_piece(*v3)
+        quantize_out(*v2)
+        store_codes(*v2)
+        quantize_out(*s0)
+        quantize_out(*v3)
+        store_codes(v3[0], s0[1])
+        quantize_out(*s1)
+        quantize_out(*s2)
+        store_codes(s1[0], s2[1])
         for q in range(4):
-            nc.scalar.dma_start(out_2[0, 4 * q : 4 * q + 4, :].bitcast(I32), out_sc[32 * q : 32 * q + 4, :].bitcast(I32))
+            queue = nc.scalar if q < 3 else nc.sync
+            queue.dma_start(out_2[0, 4 * q : 4 * q + 4, :].bitcast(I32), out_sc[32 * q : 32 * q + 4, :].bitcast(I32))

@@ -25,8 +25,9 @@ NCH = J // CH
 LAST = NCH - 1
 WD8_ROW = 4
 KIB = 1024
-AREA_A, AREA_B, AREA_C = 0, 9 * KIB, 18 * KIB
-SPLIT = 1408
+PAGE2_AT, FIRST_Y_AT, PAGE3_AT = 0, 7 * KIB, 8 * KIB
+WD_AT = 16 * KIB
+SPLIT = 1024
 
 
 def tile_list_modp_gelu_mix_resP_kernel(
@@ -57,38 +58,41 @@ def tile_list_modp_gelu_mix_resP_kernel(
 
         tab_sc = kept([P, T], U8, "tab_sc")
         wu_sc_raw = kept([P, R], U8, "wu_sc_raw")
-        wd_sc_raw = laid([P, N], U8, "wd_sc_raw", AREA_B)
-        nc.vector.memset(wu_sc_raw[:].bitcast(I32), 0)
-        nc.vector.memset(tab_sc[:].bitcast(I32), 0)
+        wd_sc_raw = kept([P, N], U8, "wd_sc_raw")
+        nc.gpsimd.memset(tab_sc[:].bitcast(I32), 0)
         nc.vector.memset(wd_sc_raw[:].bitcast(I32), 0)
+        nc.vector.memset(wu_sc_raw[:].bitcast(I32), 0)
+        pages = {0: kept([P, T], F32, "page0")}
+        nc.vector.memset(pages[0][:], 0.0)
 
-        def load_scale_rows(tile, first, rows):
-            for q in range(4):
-                nc.sync.dma_start(
+        def load_scale_rows(queue, tile, first, rows, quadrants):
+            for q in quadrants:
+                queue.dma_start(
                     tile[32 * q + first : 32 * q + first + 4, :].bitcast(I32), rows[4 * q : 4 * q + 4, :].bitcast(I32)
                 )
 
         tab_w = kept([P, T], U32, "tab_w")
-        wu_raw = laid([P, 2 * R], U8, "wu_raw", AREA_A)
-        wd8_raw = laid([P, N], I32, "wd8_raw", AREA_C + KIB)
-        wd4_raw = laid([P, 2 * N], U8, "wd4_raw", AREA_C)
+        wu_raw = kept([P, 2 * R], U8, "wu_raw")
+        wd8_raw = laid([P, N], I32, "wd8_raw", WD_AT + KIB)
+        wd4_raw = laid([P, 2 * N], U8, "wd4_raw", WD_AT)
         sm_sb = kept([P, 2, 4], F32, "sm_sb")
         wgo_sb = kept([P, J], F32, "wgo_sb")
         res = [kept([P, T], F32, "res%d" % t) for t in range(4)]
         rT_planes = rT.rearrange("(p t) c -> p t c", t=4)
+        nc.gpsimd.dma_start(sm_sb[:], sm.rearrange("(a p t) -> p a t", a=2, t=4))
         nc.sync.dma_start(offsets[:], offs)
-        nc.sync.dma_start(sm_sb[:], sm.rearrange("(a p t) -> p a t", a=2, t=4))
         nc.sync.dma_start(wu_raw[:].bitcast(I32), wu_words[0].bitcast(I32))
-        load_scale_rows(wu_sc_raw, 0, wu_scales[0])
+        load_scale_rows(nc.sync, tab_sc, 0, tab_scales[0], range(4))
         nc.sync.dma_start(tab_w[:].bitcast(I32), tab_words[0].rearrange("p t i -> p (t i)").bitcast(I32))
-        load_scale_rows(tab_sc, 0, tab_scales[0])
+        load_scale_rows(nc.sync, wu_sc_raw, 0, wu_scales[0], range(4))
         nc.sync.dma_start(wd8_raw[:], wd8_words[0].rearrange("p n i -> p (n i)").bitcast(I32))
         nc.sync.dma_start(wd4_raw[:].bitcast(I32), wd4_words[0].bitcast(I32))
-        load_scale_rows(wd_sc_raw, 0, wd4_scales[0])
-        load_scale_rows(wd_sc_raw, WD8_ROW, wd8_scales[0])
+        load_scale_rows(nc.sync, wd_sc_raw, 0, wd4_scales[0], range(4))
+        load_scale_rows(nc.sync, wd_sc_raw, WD8_ROW, wd8_scales[0], range(4))
         nc.sync.dma_start(res[0][:], rT_planes[:, 0, :])
+        nc.sync.dma_start(res[1][:], rT_planes[:, 1, :])
         nc.sync.dma_start(wgo_sb[:], wgo)
-        for t in range(1, 4):
+        for t in (2, 3):
             nc.sync.dma_start(res[t][:], rT_planes[:, t, :])
 
         def deal(dst, src):
@@ -97,22 +101,25 @@ def tile_list_modp_gelu_mix_resP_kernel(
         def weave_on_scalar(dst, planes):
             nc.scalar.copy(dst.rearrange("p (c i) t -> p c t i", i=4), planes.rearrange("p t (c i) -> p c t i", i=4))
 
+        got_sc = kept([P, J], U8, "got_sc")
         got_w = {}
-        got_sc = {}
 
-        def gather_table(c, words, scales):
-            got_w[c], got_sc[c] = words, scales
-            nc.vector.tensor_copy(scales[:], tab_sc[:].indirect(picks(c)))
-            nc.vector.tensor_copy(words[:], tab_w[:].indirect(picks(c)))
+        def gather_words(first, chunks, on):
+            words = kept([P, chunks * CH], U32, "got_w%d" % first, on)
+            entries = offsets[:, first * CH // 16 : (first + chunks) * CH // 16]
+            nc.vector.tensor_copy(words[:], tab_w[:].indirect(entries))
+            for c in range(chunks):
+                got_w[first + c] = words[:, c * CH : (c + 1) * CH]
 
-        wu = [kept([P, 2 * PASS], U8, "wu%d" % a) for a in range(2)]
+        wu = kept([P, 2 * R], U8, "wu")
         wu_sc = [kept([P, PASS], U8, "wu_sc%d" % a) for a in range(2)]
 
         def up_matmul(out, c, a, t, cols):
             nc.tensor.matmul_mx(
-                out, lhsT=wu[a][:, 2 * P * t : 2 * P * (t + 1)].bitcast(E2M1),
+                out, lhsT=wu[:, 2 * P * (4 * a + t) : 2 * P * (4 * a + t + 1)].bitcast(E2M1),
                 lhsT_scale=wu_sc[a][:, P * t : P * (t + 1)],
-                rhs=got_w[c][:, cols].bitcast(E4M3), rhs_scale=got_sc[c][:, cols], start=True, stop=True,
+                rhs=got_w[c][:, cols].bitcast(E4M3), rhs_scale=got_sc[:, c * CH : (c + 1) * CH][:, cols],
+                start=True, stop=True,
             )
 
         def down_matmuls(out, t, words, scales):
@@ -132,42 +139,45 @@ def tile_list_modp_gelu_mix_resP_kernel(
                 in_=woven_h.rearrange("p a j t -> p (a j t)"),
             )
 
-        def down_bank(c, u):
-            return 4 + 2 * (c % 2) + u
-
         h_in = {}
+        h_planes = {}
         y = {}
 
-        def hidden_pass(c, a):
-            if a == 0:
-                h_in[c] = kept([P, 2, CH, 4], BF16, "h_in%d" % c)
-            h_planes = kept([P, 4, CH], BF16, "h_planes%d%d" % (c, a))
+        def activate(c, a, banks, spent=None):
+            h_planes[c, a] = kept([P, 4, CH], BF16, "h_planes%d%d" % (c, a))
             for u in range(2):
-                bank = bank_tile([P, 2, CH], 2 * (c % 2) + u if a == 0 else down_bank(c - 1, u))
+                bank = bank_tile([P, 2, CH], banks[u])
                 for e in range(2):
                     up_matmul(bank[:, e, :], c, a, 2 * u + e, slice(0, CH))
-                act = ring.tile([P, 2, CH], F32, name="act", tag="act")
-                nc.scalar.activation(act[:], bank[:], GELU)
+                if spent is None or u == 1:
+                    act = kept([P, 2, CH], F32, "act%d%d%d" % (c, a, u))[:]
+                else:
+                    act = high_pair(c - 1)
+                nc.scalar.activation(act, bank[:], GELU)
                 for e in range(2):
                     t = 2 * u + e
-                    nc.scalar.activation(h_planes[:, t, :], act[:, e, :], COPY, scale=sm_sb[:, a, t : t + 1])
-            weave_on_scalar(h_in[c][:, a], h_planes[:])
+                    nc.scalar.activation(h_planes[c, a][:, t, :], act[:, e, :], COPY, scale=sm_sb[:, a, t : t + 1])
+                if spent is not None and u == 0:
+                    nc.scalar.copy(act, spent[:])
 
-        def empty_down(c, banks):
-            if c < LAST:
-                hidden_pass(c + 1, 0)
-            on = "h_planes%d0" % (c + 1) if c < LAST else None
-            y[c] = [kept([P, 2, CH], F32, "y%d0" % c, on), kept([P, 2, CH], F32, "y%d1" % c)]
-            for u in range(2):
-                nc.scalar.copy(y[c][u][:], banks[u][:])
-            if c < LAST:
-                hidden_pass(c + 1, 1)
+        y_high = kept([P, 2, LAST * CH], F32, "y_high")
+
+        def high_pair(c):
+            return y_high[:, :, (c - 1) * CH : c * CH]
+
+        def empty_low(c, bank, on):
+            low = kept([P, 2, CH], F32, "y_low%d" % c, on)
+            nc.scalar.copy(low[:], bank[:])
+            y[c] = [low[:, 0, :], low[:, 1, :], high_pair(c)[:, 0, :], high_pair(c)[:, 1, :]]
+
+        def weave_hidden(c, a):
+            weave_on_scalar(h_in[c][:, a], h_planes[c, a][:])
 
         def down(c):
             h_w = ring.tile([P, 2, CH], U32, name="h_w", tag="h_w", align_bytes=64)
             h_sc = ring.tile([P, 2, CH], U8, name="h_sc", tag="h_sc", align_bytes=64)
             quantize_h(h_w[:], h_sc[:], h_in[c][:])
-            banks = [bank_tile([P, 2, CH], down_bank(c, u)) for u in range(2)]
+            banks = [bank_tile([P, 2, CH], 4 + 2 * (c % 2) + u) for u in range(2)]
             for t in range(4):
                 for half in range(2):
                     cols = slice(P * half, P * (half + 1))
@@ -175,109 +185,144 @@ def tile_list_modp_gelu_mix_resP_kernel(
                         banks[t // 2][:, t % 2, cols], t,
                         [h_w[:, a, cols] for a in range(2)], [h_sc[:, a, cols] for a in range(2)],
                     )
-            empty_down(c, banks)
+            return banks
 
+        def woven_gelu(c, a, half, b, act):
+            bank = bank_tile([P, 4, P], b)
+            for t in range(4):
+                up_matmul(bank[:, t, :], c, a, t, slice(P * half, P * (half + 1)))
+            nc.scalar.activation(act, bank[:].rearrange("p t j -> p j t"), GELU)
+
+        def smooth(dst, act, a):
+            nc.vector.tensor_tensor(dst, act, sm_sb[:, a, :].unsqueeze(1).to_broadcast(list(act.shape)), MULT)
+
+        nc.vector.tensor_copy(
+            wu[:].bitcast(U16).rearrange("p (a t m) -> p a t m", a=2, t=4),
+            wu_raw[:].bitcast(U16).rearrange("p (a m t) -> p a t m", a=2, t=4),
+        )
+        nc.vector.tensor_copy(got_sc[:], tab_sc[:].indirect(offsets[:]))
+        gather_words(0, 1, None)
         for a in range(2):
-            deal(wu[a][:].bitcast(U16), wu_raw[:].bitcast(U16)[:, PASS * a : PASS * (a + 1)])
             deal(wu_sc[a][:], wu_sc_raw[:, PASS * a : PASS * (a + 1)])
-        gather_table(0, kept([P, CH], U32, "got_w0"), kept([P, CH], U8, "got_sc0"))
         act_first = {}
         for half in range(2):
             for a in range(2):
-                bank = bank_tile([P, 4, P], 2 * half + a)
-                for t in range(4):
-                    up_matmul(bank[:, t, :], 0, a, t, slice(P * half, P * (half + 1)))
-                act_first[half, a] = kept([P, P, 4], F32, "act_first%d%d" % (half, a))
-                nc.scalar.activation(act_first[half, a][:], bank[:].rearrange("p t j -> p j t"), GELU)
-
-        def smooth_first(half, woven_h):
-            for a in range(2):
-                factors = sm_sb[:, a, :].unsqueeze(1).to_broadcast([P, P, 4])
-                nc.vector.tensor_tensor(woven_h[:, a], act_first[half, a][:], factors, MULT)
-
-        pages = {}
-        gather_table(1, laid([P, CH], U32, "got_w1", AREA_A), kept([P, CH], U8, "got_sc1", "wu_sc_raw"))
-        pages[1] = laid([P, T], F32, "page1", AREA_A + KIB)
-        nc.gpsimd.memset(pages[1][:], 0.0)
+                act_first[half, a] = kept([P, P, 4], F32, "act_woven0%d%d" % (half, a))[:]
+                woven_gelu(0, a, half, 2 * half + a, act_first[half, a])
+        gather_words(1, 1, "wu_sc_raw")
         wd8 = kept([P, N], I32, "wd8")
         wd4 = kept([P, 2 * N], U8, "wd4")
-        wd_sc = kept([P, N], U8, "wd_sc", "got_w0")
-        deal(wd8[:], wd8_raw[:])
+        nc.vector.tensor_copy(
+            wd8[:].rearrange("p (t m i) -> p m t i", t=4, i=4), wd8_raw[:].rearrange("p (m i t) -> p m t i", t=4, i=4)
+        )
         deal(wd4[:].bitcast(U16), wd4_raw[:].bitcast(U16))
-        h_first = [laid([P, 2, P, 4], BF16, "h_first0", AREA_C)]
-        smooth_first(0, h_first[0])
-        deal(wd_sc[:], wd_sc_raw[:])
-        h_first.append(laid([P, 2, P, 4], BF16, "h_first1", AREA_B))
-        smooth_first(1, h_first[1])
-        first_banks = [bank_tile([P, 2, CH], down_bank(0, u)) for u in range(2)]
+        first_banks = [bank_tile([P, 2, CH], 4 + u) for u in range(2)]
         for half in range(2):
+            if half == 0:
+                h_first = laid([P, 2, P, 4], BF16, "h_first0", WD_AT)
+            else:
+                h_first = kept([P, 2, P, 4], BF16, "h_first1", "wd_sc_raw")
+            for a in range(2):
+                smooth(h_first[:, a], act_first[half, a], a)
+            if half == 0:
+                wd_sc = kept([P, N], U8, "wd_sc", "act_woven001")
+                deal(wd_sc[:], wd_sc_raw[:])
             h_w_first = kept([P, 2, P], U32, "h_w_first%d" % half)
             h_sc_first = kept([P, 2, P], U8, "h_sc_first%d" % half)
-            quantize_h(h_w_first[:], h_sc_first[:], h_first[half][:])
+            quantize_h(h_w_first[:], h_sc_first[:], h_first[:])
             for t in range(4):
                 down_matmuls(
                     first_banks[t // 2][:, t % 2, P * half : P * (half + 1)], t,
                     [h_w_first[:, a, :] for a in range(2)], [h_sc_first[:, a, :] for a in range(2)],
                 )
-        empty_down(0, first_banks)
-        gather_table(2, kept([P, CH], U32, "got_w2", "act_first11"), kept([P, CH], U8, "got_sc2", "act_first10"))
-        gather_table(3, laid([P, CH], U32, "got_w3", AREA_B), laid([P, CH], U8, "got_sc3", AREA_C))
-        pages[0] = kept([P, T], F32, "page0")
-        nc.vector.memset(pages[0][:], 0.0)
-        pages[2] = laid([P, T], F32, "page2", AREA_B + KIB)
-        nc.gpsimd.memset(pages[2][:], 0.0)
-        pages[3] = kept([P, T], F32, "page3", "tab_w")
-        nc.gpsimd.memset(pages[3][:], 0.0)
+        first_y = [laid([P, 2, CH], F32, "first_y0", FIRST_Y_AT), kept([P, 2, CH], F32, "first_y1")]
+        y[0] = [first_y[t // 2][:, t % 2, :] for t in range(4)]
+        for u in range(2):
+            nc.scalar.copy(first_y[u][:], first_banks[u][:])
+        for c in range(1, NCH):
+            h_in[c] = kept([P, 2, CH, 4], BF16, "h_in%d" % c)
+        activate(1, 0, (0, 1))
+        weave_hidden(1, 0)
+        activate(1, 1, (4, 2))
+        weave_hidden(1, 1)
+        gather_words(2, 2, "wd_sc_raw")
+        pages[1] = kept([P, T], F32, "page1", "tab_w")
+        nc.gpsimd.memset(pages[1][:], 0.0)
 
         def add_residual(c, t, total):
-            nc.vector.tensor_tensor(total, res[t][:].indirect(picks(c)), y[c][t // 2][:, t % 2, :], ADD)
+            nc.vector.tensor_tensor(total, res[t][:].indirect(picks(c)), y[c][t], ADD)
 
         def scatter(c, t, total):
             nc.vector.tensor_tensor(pages[t][:].indirect(picks(c)), total, wgo_sb[:, c * CH : (c + 1) * CH], MULT)
 
         def fresh_totals():
-            totals = ring.tile([P, 2, CH], F32, name="totals", tag="totals")
+            totals = ring.tile([P, 4, CH], F32, name="totals", tag="totals")
             return totals[:]
 
         out_planes = out_0.rearrange("(p t) c -> p t c", t=4)
-        pairs = kept([P, 2, SPLIT, 2], BF16, "pairs")
-        rounded = kept([P, 4, T - SPLIT], BF16, "rounded")
+        pairs = kept([P, 2, T, 2], BF16, "pairs")
 
         def finish_plane(t):
             nc.sync.dma_start(out_planes[:, t, :], pages[t][:])
             if t < 2:
-                nc.scalar.copy(pairs[:, 0, :, t], pages[t][:, 0:SPLIT])
+                nc.scalar.copy(pairs[:, 0, :, t], pages[t][:])
             if t == 2:
-                nc.scalar.copy(pairs[:, 1], pages[t][:, 0:SPLIT].unsqueeze(2).to_broadcast([P, SPLIT, 2]))
-            if t < 3:
-                nc.scalar.copy(rounded[:, t, :], pages[t][:, SPLIT:T])
+                nc.scalar.copy(pairs[:, 1, 0:SPLIT], pages[t][:, 0:SPLIT].unsqueeze(2).to_broadcast([P, SPLIT, 2]))
+                nc.scalar.copy(pairs[:, 1, SPLIT:T, 0], pages[t][:, SPLIT:T])
 
-        for c in range(LAST):
-            totals = fresh_totals()
-            for t in (0, 1):
-                add_residual(c, t, totals[:, t, :])
-            for t in (0, 1):
-                scatter(c, t, totals[:, t, :])
-            down(c + 1)
-            spent = h_in[c + 1][:, 0].rearrange("p j t -> p (j t)").bitcast(F32).rearrange("p (e j) -> p e j", e=2)
-            planes = (2, 3) if c < LAST - 1 else (2,)
-            for t in planes:
-                add_residual(c, t, spent[:, t - 2, :])
-            for t in planes:
-                scatter(c, t, spent[:, t - 2, :])
-        low, high = fresh_totals(), fresh_totals()
+        def pair_of_units(first, second, totals):
+            add_residual(*first, totals[:, 0, :])
+            add_residual(*second, totals[:, 1, :])
+            scatter(*first, totals[:, 0, :])
+            scatter(*second, totals[:, 1, :])
+
+        def after_weave(c):
+            return kept([P, 2, CH], F32, "late%d" % c, "h_planes%d1" % c)
+
+        totals = fresh_totals()
         for t in (0, 1):
-            add_residual(LAST, t, low[:, t, :])
+            add_residual(0, t, totals[:, t, :])
+        pages[2] = laid([P, T], F32, "page2", PAGE2_AT)
+        nc.gpsimd.memset(pages[2][:], 0.0)
         for t in (0, 1):
-            scatter(LAST, t, low[:, t, :])
-            finish_plane(t)
-        for t in (2, 3):
-            add_residual(LAST, t, high[:, t - 2, :])
-        scatter(LAST, 2, high[:, 0, :])
+            scatter(0, t, totals[:, t, :])
+
+        def next_hidden(c, banks):
+            activate(c, 0, (0, 1))
+            weave_hidden(c, 0)
+            empty_low(c - 1, banks[0], "h_planes%d0" % c)
+            activate(c, 1, (2, 3), banks[1])
+            weave_hidden(c, 1)
+
+        next_hidden(2, down(1))
+        pages[3] = kept([P, T], F32, "page3", "h_in1")
+        nc.gpsimd.memset(pages[3][:], 0.0)
+        pair_of_units((0, 2), (0, 3), after_weave(1))
+        for c in (1, 2):
+            pair_of_units((c, 0), (c, 1), fresh_totals())
+            banks = down(c + 1)
+            if c + 1 < LAST:
+                next_hidden(c + 2, banks)
+            else:
+                empty_low(LAST, banks[0], None)
+                nc.scalar.copy(high_pair(LAST), banks[1][:])
+            late = after_weave(c + 1)
+            add_residual(c, 2, late[:, 0, :])
+            scatter(c, 2, late[:, 0, :])
+        last = kept([P, 5 * CH], F32, "last")
+        totals = [last[:, (2 + t) * CH : (3 + t) * CH] for t in range(3)]
+        for t in (0, 1):
+            add_residual(LAST, t, totals[t])
+        scatter(LAST, 0, totals[0])
+        finish_plane(0)
+        add_residual(LAST, 2, totals[2])
+        scatter(LAST, 1, totals[1])
+        finish_plane(1)
+        later = offsets[:, CH // 16 : J // 16]
+        nc.vector.tensor_tensor(last[:, 0 : LAST * CH], res[3][:].indirect(later), y_high[:, 1, :], ADD)
+        scatter(LAST, 2, totals[2])
         finish_plane(2)
-        add_residual(LAST - 1, 3, low[:, 1, :])
-        scatter(LAST, 3, high[:, 1, :])
-        scatter(LAST - 1, 3, low[:, 1, :])
+        nc.vector.tensor_tensor(pages[3][:].indirect(later), last[:, 0 : LAST * CH], wgo_sb[:, CH:J], MULT)
         finish_plane(3)
 
         out_w = kept([P, T], U32, "out_w")
@@ -286,17 +331,16 @@ def tile_list_modp_gelu_mix_resP_kernel(
         pair_words = pairs[:].rearrange("p u c e -> p u (c e)").bitcast(F32)
         woven = {}
 
-        def vector_piece(lo, hi):
+        def woven_words(lo, hi):
             woven[lo] = kept([P, hi - lo, 4], BF16, "woven%d" % lo)
-            nc.vector.tensor_copy(
-                woven[lo][:].rearrange("p c t -> p (c t)").bitcast(F32).rearrange("p (c u) -> p c u", u=2),
-                pair_words[:, :, lo:hi].rearrange("p u c -> p c u"),
-            )
+            return woven[lo][:].rearrange("p c t -> p (c t)").bitcast(F32).rearrange("p (c u) -> p c u", u=2)
+
+        def vector_piece(lo, hi):
+            nc.vector.tensor_copy(woven_words(lo, hi), pair_words[:, :, lo:hi].rearrange("p u c -> p c u"))
 
         def scalar_piece(lo, hi):
-            woven[lo] = kept([P, hi - lo, 4], BF16, "woven%d" % lo)
-            nc.scalar.copy(rounded[:, 3, lo - SPLIT : hi - SPLIT], pages[3][:, lo:hi])
-            weave_on_scalar(woven[lo][:], rounded[:, :, lo - SPLIT : hi - SPLIT])
+            nc.scalar.copy(pairs[:, 1, lo:hi, 1], pages[3][:, lo:hi])
+            nc.scalar.copy(woven_words(lo, hi), pair_words[:, :, lo:hi].rearrange("p u c -> p c u"))
 
         def quantize_out(lo, hi):
             nc.vector.quantize_mx(
@@ -306,26 +350,19 @@ def tile_list_modp_gelu_mix_resP_kernel(
         def store_codes(lo, hi):
             nc.sync.dma_start(out_words[:, lo:hi], out_w[:, lo:hi].bitcast(I32))
 
-        v0, v1, v2, v3 = (0, 256), (256, 768), (768, 1280), (1280, SPLIT)
-        s0, s1, s2 = (SPLIT, 1664), (1664, 1920), (1920, T)
-        nc.vector.tensor_copy(pairs[:, 1, v0[0] : v1[1], 1], pages[3][:, v0[0] : v1[1]])
-        nc.vector.tensor_copy(pairs[:, 1, v2[0] : v3[1], 1], pages[3][:, v2[0] : v3[1]])
+        v0, v1 = (0, 512), (512, SPLIT)
+        s0, s1, s2 = (SPLIT, 1536), (1536, 1792), (1792, T)
+        for lo, hi in (v0, v1):
+            nc.vector.tensor_copy(pairs[:, 1, lo:hi, 1], pages[3][:, lo:hi])
         for piece in (s0, s1, s2):
             scalar_piece(*piece)
         vector_piece(*v0)
         vector_piece(*v1)
-        quantize_out(*v0)
-        vector_piece(*v2)
-        quantize_out(*v1)
-        store_codes(v0[0], v1[1])
-        vector_piece(*v3)
-        quantize_out(*v2)
-        store_codes(*v2)
-        quantize_out(*s0)
-        quantize_out(*v3)
-        store_codes(v3[0], s0[1])
-        quantize_out(*s1)
-        quantize_out(*s2)
+        for piece in (v0, v1, s0):
+            quantize_out(*piece)
+            store_codes(*piece)
+        for piece in (s1, s2):
+            quantize_out(*piece)
         store_codes(s1[0], s2[1])
         for q in range(4):
             queue = nc.scalar if q < 3 else nc.sync

@@ -143,22 +143,19 @@ def tile_list_modp_gelu_mix_resP_kernel(
         h_planes = {}
         y = {}
 
-        def activate(c, a, banks, spent=None):
-            h_planes[c, a] = kept([P, 4, CH], BF16, "h_planes%d%d" % (c, a))
-            for u in range(2):
-                bank = bank_tile([P, 2, CH], banks[u])
-                for e in range(2):
-                    up_matmul(bank[:, e, :], c, a, 2 * u + e, slice(0, CH))
-                if spent is None or u == 1:
-                    act = kept([P, 2, CH], F32, "act%d%d%d" % (c, a, u))[:]
-                else:
-                    act = high_pair(c - 1)
-                nc.scalar.activation(act, bank[:], GELU)
-                for e in range(2):
-                    t = 2 * u + e
-                    nc.scalar.activation(h_planes[c, a][:, t, :], act[:, e, :], COPY, scale=sm_sb[:, a, t : t + 1])
-                if spent is not None and u == 0:
-                    nc.scalar.copy(act, spent[:])
+        acts = {}
+
+        def gelu_pair(c, a, u, b, act=None):
+            bank = bank_tile([P, 2, CH], b)
+            for e in range(2):
+                up_matmul(bank[:, e, :], c, a, 2 * u + e, slice(0, CH))
+            acts[c, a, u] = act if act is not None else kept([P, 2, CH], F32, "act%d%d%d" % (c, a, u))[:]
+            nc.scalar.activation(acts[c, a, u], bank[:], GELU)
+
+        def scale_plane(c, a, t):
+            if t == 0:
+                h_planes[c, a] = kept([P, 4, CH], BF16, "h_planes%d%d" % (c, a))
+            nc.scalar.activation(h_planes[c, a][:, t, :], acts[c, a, t // 2][:, t % 2, :], COPY, scale=sm_sb[:, a, t : t + 1])
 
         y_high = kept([P, 2, LAST * CH], F32, "y_high")
 
@@ -209,13 +206,13 @@ def tile_list_modp_gelu_mix_resP_kernel(
             for a in range(2):
                 act_first[half, a] = kept([P, P, 4], F32, "act_woven0%d%d" % (half, a))[:]
                 woven_gelu(0, a, half, 2 * half + a, act_first[half, a])
-        gather_words(1, 1, "wu_sc_raw")
         wd8 = kept([P, N], I32, "wd8")
         wd4 = kept([P, 2 * N], U8, "wd4")
         nc.vector.tensor_copy(
             wd8[:].rearrange("p (t m i) -> p m t i", t=4, i=4), wd8_raw[:].rearrange("p (m i t) -> p m t i", t=4, i=4)
         )
         deal(wd4[:].bitcast(U16), wd4_raw[:].bitcast(U16))
+        gather_words(1, 1, "wu_sc_raw")
         first_banks = [bank_tile([P, 2, CH], 4 + u) for u in range(2)]
         for half in range(2):
             if half == 0:
@@ -225,7 +222,7 @@ def tile_list_modp_gelu_mix_resP_kernel(
             for a in range(2):
                 smooth(h_first[:, a], act_first[half, a], a)
             if half == 0:
-                wd_sc = kept([P, N], U8, "wd_sc", "act_woven001")
+                wd_sc = kept([P, N], U8, "wd_sc", "act_woven000")
                 deal(wd_sc[:], wd_sc_raw[:])
             h_w_first = kept([P, 2, P], U32, "h_w_first%d" % half)
             h_sc_first = kept([P, 2, P], U8, "h_sc_first%d" % half)
@@ -241,11 +238,18 @@ def tile_list_modp_gelu_mix_resP_kernel(
             nc.scalar.copy(first_y[u][:], first_banks[u][:])
         for c in range(1, NCH):
             h_in[c] = kept([P, 2, CH, 4], BF16, "h_in%d" % c)
-        activate(1, 0, (0, 1))
+        gelu_pair(1, 0, 0, 0)
+        gelu_pair(1, 0, 1, 1)
+        for t in range(4):
+            scale_plane(1, 0, t)
+        gelu_pair(1, 1, 0, 4)
         weave_hidden(1, 0)
-        activate(1, 1, (4, 2))
-        weave_hidden(1, 1)
+        gelu_pair(1, 1, 1, 5)
+        for t in range(4):
+            scale_plane(1, 1, t)
         gather_words(2, 2, "wd_sc_raw")
+        gelu_pair(2, 0, 0, 0)
+        weave_hidden(1, 1)
         pages[1] = kept([P, T], F32, "page1", "tab_w")
         nc.gpsimd.memset(pages[1][:], 0.0)
 
@@ -283,21 +287,34 @@ def tile_list_modp_gelu_mix_resP_kernel(
         for t in (0, 1):
             add_residual(0, t, totals[:, t, :])
         pages[2] = laid([P, T], F32, "page2", PAGE2_AT)
-        nc.gpsimd.memset(pages[2][:], 0.0)
-        for t in (0, 1):
+        pages[3] = laid([P, T], F32, "page3", PAGE3_AT)
+        for t in (2, 3):
+            nc.gpsimd.memset(pages[t][:], 0.0)
+        scatter(0, 0, totals[:, 0, :])
+        add_residual(0, 2, totals[:, 2, :])
+        for t in (1, 2):
             scatter(0, t, totals[:, t, :])
 
         def next_hidden(c, banks):
-            activate(c, 0, (0, 1))
+            gelu_pair(c, 0, 1, 1)
+            for t in range(4):
+                scale_plane(c, 0, t)
+            gelu_pair(c, 1, 0, 2, high_pair(c - 1))
+            empty_low(c - 1, banks[0], "act%d01" % c)
             weave_hidden(c, 0)
-            empty_low(c - 1, banks[0], "h_planes%d0" % c)
-            activate(c, 1, (2, 3), banks[1])
+            gelu_pair(c, 1, 1, 3)
+            for t in range(3):
+                scale_plane(c, 1, t)
+            nc.scalar.copy(high_pair(c - 1), banks[1][:])
+            scale_plane(c, 1, 3)
+            if c < LAST:
+                gelu_pair(c + 1, 0, 0, 0)
             weave_hidden(c, 1)
 
         next_hidden(2, down(1))
-        pages[3] = kept([P, T], F32, "page3", "h_in1")
-        nc.gpsimd.memset(pages[3][:], 0.0)
-        pair_of_units((0, 2), (0, 3), after_weave(1))
+        late = after_weave(1)
+        add_residual(0, 3, late[:, 0, :])
+        scatter(0, 3, late[:, 0, :])
         for c in (1, 2):
             pair_of_units((c, 0), (c, 1), fresh_totals())
             banks = down(c + 1)
@@ -326,7 +343,7 @@ def tile_list_modp_gelu_mix_resP_kernel(
         finish_plane(3)
 
         out_w = kept([P, T], U32, "out_w")
-        out_sc = kept([P, T], U8, "out_sc")
+        out_sc = kept([P, T // 2], U8, "out_sc")
         out_words = out_1[0].rearrange("p t i -> p (t i)").bitcast(I32)
         pair_words = pairs[:].rearrange("p u c e -> p u (c e)").bitcast(F32)
         woven = {}
@@ -338,13 +355,18 @@ def tile_list_modp_gelu_mix_resP_kernel(
         def vector_piece(lo, hi):
             nc.vector.tensor_copy(woven_words(lo, hi), pair_words[:, :, lo:hi].rearrange("p u c -> p c u"))
 
-        def scalar_piece(lo, hi):
+        def scalar_round(lo, hi):
             nc.scalar.copy(pairs[:, 1, lo:hi, 1], pages[3][:, lo:hi])
+
+        def scalar_weave(lo, hi):
             nc.scalar.copy(woven_words(lo, hi), pair_words[:, :, lo:hi].rearrange("p u c -> p c u"))
 
         def quantize_out(lo, hi):
+            side = lo // (T // 2)
             nc.vector.quantize_mx(
-                out=out_w[:, lo:hi].bitcast(E4M3), scales=out_sc[:, lo:hi], in_=woven[lo][:].rearrange("p c t -> p (c t)")
+                out=out_w[:, lo:hi].bitcast(E4M3),
+                scales=out_sc[4 * side : P, lo - side * T // 2 : hi - side * T // 2],
+                in_=woven[lo][:].rearrange("p c t -> p (c t)"),
             )
 
         def store_codes(lo, hi):
@@ -354,16 +376,16 @@ def tile_list_modp_gelu_mix_resP_kernel(
         s0, s1, s2 = (SPLIT, 1536), (1536, 1792), (1792, T)
         for lo, hi in (v0, v1):
             nc.vector.tensor_copy(pairs[:, 1, lo:hi, 1], pages[3][:, lo:hi])
+        scalar_round(*s0)
+        scalar_round(s1[0], s2[1])
         for piece in (s0, s1, s2):
-            scalar_piece(*piece)
+            scalar_weave(*piece)
         vector_piece(*v0)
         vector_piece(*v1)
-        for piece in (v0, v1, s0):
+        for piece in (v0, v1, s0, s1, s2):
             quantize_out(*piece)
             store_codes(*piece)
-        for piece in (s1, s2):
-            quantize_out(*piece)
-        store_codes(s1[0], s2[1])
         for q in range(4):
             queue = nc.scalar if q < 3 else nc.sync
-            queue.dma_start(out_2[0, 4 * q : 4 * q + 4, :].bitcast(I32), out_sc[32 * q : 32 * q + 4, :].bitcast(I32))
+            rows = out_2[0, 4 * q : 4 * q + 4, :].bitcast(I32).rearrange("r (side c) -> side r c", side=2)
+            queue.dma_start(rows, out_sc[32 * q : 32 * q + 8, :].bitcast(I32))

@@ -98,9 +98,6 @@ def tile_list_modp_gelu_mix_resP_kernel(
         def deal(dst, src):
             nc.vector.tensor_copy(dst.rearrange("p (t m) -> p t m", t=4), src.rearrange("p (m t) -> p t m", t=4))
 
-        def weave_on_scalar(dst, planes):
-            nc.scalar.copy(dst.rearrange("p (c i) t -> p c t i", i=4), planes.rearrange("p t (c i) -> p c t i", i=4))
-
         got_sc = kept([P, J], U8, "got_sc")
         got_w = {}
 
@@ -154,8 +151,8 @@ def tile_list_modp_gelu_mix_resP_kernel(
 
         def scale_plane(c, a, t):
             if t == 0:
-                h_planes[c, a] = kept([P, 4, CH], BF16, "h_planes%d%d" % (c, a))
-            nc.scalar.activation(h_planes[c, a][:, t, :], acts[c, a, t // 2][:, t % 2, :], COPY, scale=sm_sb[:, a, t : t + 1])
+                h_planes[c, a] = kept([P, 2, CH, 2], BF16, "h_planes%d%d" % (c, a))
+            nc.scalar.activation(h_planes[c, a][:, t // 2, :, t % 2], acts[c, a, t // 2][:, t % 2, :], COPY, scale=sm_sb[:, a, t : t + 1])
 
         y_high = kept([P, 2, LAST * CH], F32, "y_high")
 
@@ -168,7 +165,10 @@ def tile_list_modp_gelu_mix_resP_kernel(
             y[c] = [low[:, 0, :], low[:, 1, :], high_pair(c)[:, 0, :], high_pair(c)[:, 1, :]]
 
         def weave_hidden(c, a):
-            weave_on_scalar(h_in[c][:, a], h_planes[c, a][:])
+            nc.scalar.copy(
+                h_in[c][:, a].rearrange("p j t -> p (j t)").bitcast(F32).rearrange("p (j u) -> p j u", u=2),
+                h_planes[c, a][:].rearrange("p u j e -> p u (j e)").bitcast(F32).rearrange("p u j -> p j u"),
+            )
 
         def down(c):
             h_w = ring.tile([P, 2, CH], U32, name="h_w", tag="h_w", align_bytes=64)
@@ -287,12 +287,8 @@ def tile_list_modp_gelu_mix_resP_kernel(
         for t in (0, 1):
             add_residual(0, t, totals[:, t, :])
         pages[2] = laid([P, T], F32, "page2", PAGE2_AT)
-        pages[3] = laid([P, T], F32, "page3", PAGE3_AT)
-        for t in (2, 3):
-            nc.gpsimd.memset(pages[t][:], 0.0)
-        scatter(0, 0, totals[:, 0, :])
-        add_residual(0, 2, totals[:, 2, :])
-        for t in (1, 2):
+        nc.gpsimd.memset(pages[2][:], 0.0)
+        for t in (0, 1):
             scatter(0, t, totals[:, t, :])
 
         def next_hidden(c, banks):
@@ -312,9 +308,9 @@ def tile_list_modp_gelu_mix_resP_kernel(
             weave_hidden(c, 1)
 
         next_hidden(2, down(1))
-        late = after_weave(1)
-        add_residual(0, 3, late[:, 0, :])
-        scatter(0, 3, late[:, 0, :])
+        pages[3] = kept([P, T], F32, "page3", "h_in1")
+        nc.gpsimd.memset(pages[3][:], 0.0)
+        pair_of_units((0, 2), (0, 3), after_weave(1))
         for c in (1, 2):
             pair_of_units((c, 0), (c, 1), fresh_totals())
             banks = down(c + 1)

@@ -23,11 +23,14 @@ PASS = 512
 CH = 256
 NCH = J // CH
 LAST = NCH - 1
-WD8_ROW = 4
+UPPER_ROW = 4
+SCALE_ORDER = (0, 2, 1, 3)
 KIB = 1024
-PAGE2_AT, FIRST_Y_AT, PAGE3_AT = 0, 7 * KIB, 8 * KIB
+PAGE2_AT = 0
+FIRST_Y_AT = 7 * KIB
 WD_AT = 16 * KIB
-SPLIT = 1024
+LATE_AT = 19 * KIB
+SPLIT = T // 2
 
 
 def tile_list_modp_gelu_mix_resP_kernel(
@@ -53,21 +56,21 @@ def tile_list_modp_gelu_mix_resP_kernel(
 
         offsets = lists.tile([P, J // 16], U16, name="offsets")
 
-        def picks(c):
-            return offsets[:, c * CH // 16 : (c + 1) * CH // 16]
+        def picks(first, chunks=1):
+            return offsets[:, first * CH // 16 : (first + chunks) * CH // 16]
 
         tab_sc = kept([P, T], U8, "tab_sc")
         wu_sc_raw = kept([P, R], U8, "wu_sc_raw")
-        wd_sc_raw = kept([P, N], U8, "wd_sc_raw")
+        wd_sc_raw = laid([P, N], U8, "wd_sc_raw", LATE_AT)
         nc.gpsimd.memset(tab_sc[:].bitcast(I32), 0)
         nc.vector.memset(wd_sc_raw[:].bitcast(I32), 0)
         nc.vector.memset(wu_sc_raw[:].bitcast(I32), 0)
         pages = {0: kept([P, T], F32, "page0")}
         nc.vector.memset(pages[0][:], 0.0)
 
-        def load_scale_rows(queue, tile, first, rows, quadrants):
-            for q in quadrants:
-                queue.dma_start(
+        def load_scale_rows(tile, first, rows):
+            for q in range(4):
+                nc.sync.dma_start(
                     tile[32 * q + first : 32 * q + first + 4, :].bitcast(I32), rows[4 * q : 4 * q + 4, :].bitcast(I32)
                 )
 
@@ -82,13 +85,13 @@ def tile_list_modp_gelu_mix_resP_kernel(
         nc.gpsimd.dma_start(sm_sb[:], sm.rearrange("(a p t) -> p a t", a=2, t=4))
         nc.sync.dma_start(offsets[:], offs)
         nc.sync.dma_start(wu_raw[:].bitcast(I32), wu_words[0].bitcast(I32))
-        load_scale_rows(nc.sync, tab_sc, 0, tab_scales[0], range(4))
+        load_scale_rows(tab_sc, 0, tab_scales[0])
         nc.sync.dma_start(tab_w[:].bitcast(I32), tab_words[0].rearrange("p t i -> p (t i)").bitcast(I32))
-        load_scale_rows(nc.sync, wu_sc_raw, 0, wu_scales[0], range(4))
+        load_scale_rows(wu_sc_raw, 0, wu_scales[0])
         nc.sync.dma_start(wd8_raw[:], wd8_words[0].rearrange("p n i -> p (n i)").bitcast(I32))
         nc.sync.dma_start(wd4_raw[:].bitcast(I32), wd4_words[0].bitcast(I32))
-        load_scale_rows(nc.sync, wd_sc_raw, 0, wd4_scales[0], range(4))
-        load_scale_rows(nc.sync, wd_sc_raw, WD8_ROW, wd8_scales[0], range(4))
+        load_scale_rows(wd_sc_raw, 0, wd4_scales[0])
+        load_scale_rows(wd_sc_raw, UPPER_ROW, wd8_scales[0])
         nc.sync.dma_start(res[0][:], rT_planes[:, 0, :])
         nc.sync.dma_start(res[1][:], rT_planes[:, 1, :])
         nc.sync.dma_start(wgo_sb[:], wgo)
@@ -98,15 +101,13 @@ def tile_list_modp_gelu_mix_resP_kernel(
         def deal(dst, src):
             nc.vector.tensor_copy(dst.rearrange("p (t m) -> p t m", t=4), src.rearrange("p (m t) -> p t m", t=4))
 
-        got_sc = kept([P, J], U8, "got_sc")
+        got_sc = {}
         got_w = {}
 
-        def gather_words(first, chunks, on):
-            words = kept([P, chunks * CH], U32, "got_w%d" % first, on)
-            entries = offsets[:, first * CH // 16 : (first + chunks) * CH // 16]
-            nc.vector.tensor_copy(words[:], tab_w[:].indirect(entries))
+        def gather_table(got, table, first, chunks, tile):
+            nc.vector.tensor_copy(tile[:], table[:].indirect(picks(first, chunks)))
             for c in range(chunks):
-                got_w[first + c] = words[:, c * CH : (c + 1) * CH]
+                got[first + c] = tile[:, c * CH : (c + 1) * CH]
 
         wu = kept([P, 2 * R], U8, "wu")
         wu_sc = [kept([P, PASS], U8, "wu_sc%d" % a) for a in range(2)]
@@ -115,13 +116,13 @@ def tile_list_modp_gelu_mix_resP_kernel(
             nc.tensor.matmul_mx(
                 out, lhsT=wu[:, 2 * P * (4 * a + t) : 2 * P * (4 * a + t + 1)].bitcast(E2M1),
                 lhsT_scale=wu_sc[a][:, P * t : P * (t + 1)],
-                rhs=got_w[c][:, cols].bitcast(E4M3), rhs_scale=got_sc[:, c * CH : (c + 1) * CH][:, cols],
+                rhs=got_w[c][:, cols].bitcast(E4M3), rhs_scale=got_sc[c][:, cols],
                 start=True, stop=True,
             )
 
         def down_matmuls(out, t, words, scales):
             nc.tensor.matmul_mx(
-                out, lhsT=wd8[:, P * t : P * (t + 1)].bitcast(E4M3), lhsT_scale=wd_sc[WD8_ROW:P, P * t : P * (t + 1)],
+                out, lhsT=wd8[:, P * t : P * (t + 1)].bitcast(E4M3), lhsT_scale=wd_sc[UPPER_ROW:P, P * t : P * (t + 1)],
                 rhs=words[0].bitcast(E4M3), rhs_scale=scales[0], start=True, stop=False,
             )
             nc.tensor.matmul_mx(
@@ -136,11 +137,10 @@ def tile_list_modp_gelu_mix_resP_kernel(
                 in_=woven_h.rearrange("p a j t -> p (a j t)"),
             )
 
-        h_in = {}
-        h_planes = {}
-        y = {}
-
         acts = {}
+        h_pairs = {}
+        h_in = {}
+        y = {}
 
         def gelu_pair(c, a, u, b, act=None):
             bank = bank_tile([P, 2, CH], b)
@@ -149,10 +149,11 @@ def tile_list_modp_gelu_mix_resP_kernel(
             acts[c, a, u] = act if act is not None else kept([P, 2, CH], F32, "act%d%d%d" % (c, a, u))[:]
             nc.scalar.activation(acts[c, a, u], bank[:], GELU)
 
-        def scale_plane(c, a, t):
-            if t == 0:
-                h_planes[c, a] = kept([P, 2, CH, 2], BF16, "h_planes%d%d" % (c, a))
-            nc.scalar.activation(h_planes[c, a][:, t // 2, :, t % 2], acts[c, a, t // 2][:, t % 2, :], COPY, scale=sm_sb[:, a, t : t + 1])
+        def scale_planes(c, a):
+            h_pairs[c, a] = kept([P, 2, CH, 2], BF16, "h_pairs%d%d" % (c, a))
+            for t in SCALE_ORDER:
+                u, e = divmod(t, 2)
+                nc.scalar.activation(h_pairs[c, a][:, u, :, e], acts[c, a, u][:, e, :], COPY, scale=sm_sb[:, a, t : t + 1])
 
         y_high = kept([P, 2, LAST * CH], F32, "y_high")
 
@@ -167,7 +168,7 @@ def tile_list_modp_gelu_mix_resP_kernel(
         def weave_hidden(c, a):
             nc.scalar.copy(
                 h_in[c][:, a].rearrange("p j t -> p (j t)").bitcast(F32).rearrange("p (j u) -> p j u", u=2),
-                h_planes[c, a][:].rearrange("p u j e -> p u (j e)").bitcast(F32).rearrange("p u j -> p j u"),
+                h_pairs[c, a][:].rearrange("p u j e -> p u (j e)").bitcast(F32).rearrange("p u j -> p j u"),
             )
 
         def down(c):
@@ -184,70 +185,64 @@ def tile_list_modp_gelu_mix_resP_kernel(
                     )
             return banks
 
-        def woven_gelu(c, a, half, b, act):
-            bank = bank_tile([P, 4, P], b)
-            for t in range(4):
-                up_matmul(bank[:, t, :], c, a, t, slice(P * half, P * (half + 1)))
-            nc.scalar.activation(act, bank[:].rearrange("p t j -> p j t"), GELU)
-
-        def smooth(dst, act, a):
-            nc.vector.tensor_tensor(dst, act, sm_sb[:, a, :].unsqueeze(1).to_broadcast(list(act.shape)), MULT)
-
         nc.vector.tensor_copy(
             wu[:].bitcast(U16).rearrange("p (a t m) -> p a t m", a=2, t=4),
             wu_raw[:].bitcast(U16).rearrange("p (a m t) -> p a t m", a=2, t=4),
         )
-        nc.vector.tensor_copy(got_sc[:], tab_sc[:].indirect(offsets[:]))
-        gather_words(0, 1, None)
+        gather_table(got_sc, tab_sc, 0, LAST, kept([P, LAST * CH], U8, "got_sc0"))
+        gather_table(got_w, tab_w, 0, 1, kept([P, CH], U32, "got_w0"))
         for a in range(2):
             deal(wu_sc[a][:], wu_sc_raw[:, PASS * a : PASS * (a + 1)])
         act_first = {}
         for half in range(2):
             for a in range(2):
-                act_first[half, a] = kept([P, P, 4], F32, "act_woven0%d%d" % (half, a))[:]
-                woven_gelu(0, a, half, 2 * half + a, act_first[half, a])
+                act_first[half, a] = kept([P, P, 4], F32, "act_first%d%d" % (half, a))
+                bank = bank_tile([P, 4, P], 2 * half + a)
+                for t in range(4):
+                    up_matmul(bank[:, t, :], 0, a, t, slice(P * half, P * (half + 1)))
+                nc.scalar.activation(act_first[half, a][:], bank[:].rearrange("p t j -> p j t"), GELU)
         wd8 = kept([P, N], I32, "wd8")
         wd4 = kept([P, 2 * N], U8, "wd4")
         nc.vector.tensor_copy(
             wd8[:].rearrange("p (t m i) -> p m t i", t=4, i=4), wd8_raw[:].rearrange("p (m i t) -> p m t i", t=4, i=4)
         )
         deal(wd4[:].bitcast(U16), wd4_raw[:].bitcast(U16))
-        gather_words(1, 1, "wu_sc_raw")
-        first_banks = [bank_tile([P, 2, CH], 4 + u) for u in range(2)]
+        gather_table(got_w, tab_w, 1, 1, kept([P, CH], U32, "got_w1", "wu_sc_raw"))
+        first_high = bank_tile([P, 2, CH], 5)
+        first_planes = [bank_tile([P, CH], 6)[:], bank_tile([P, CH], 4)[:], first_high[:, 0, :], first_high[:, 1, :]]
         for half in range(2):
-            if half == 0:
-                h_first = laid([P, 2, P, 4], BF16, "h_first0", WD_AT)
-            else:
-                h_first = kept([P, 2, P, 4], BF16, "h_first1", "wd_sc_raw")
+            h_first = laid([P, 2, P, 4], BF16, "h_first%d" % half, (WD_AT, LATE_AT)[half])
             for a in range(2):
-                smooth(h_first[:, a], act_first[half, a], a)
+                factors = sm_sb[:, a, :].unsqueeze(1).to_broadcast([P, P, 4])
+                nc.vector.tensor_tensor(h_first[:, a], act_first[half, a][:], factors, MULT)
             if half == 0:
-                wd_sc = kept([P, N], U8, "wd_sc", "act_woven000")
+                wd_sc = kept([P, N], U8, "wd_sc", "act_first00")
                 deal(wd_sc[:], wd_sc_raw[:])
             h_w_first = kept([P, 2, P], U32, "h_w_first%d" % half)
             h_sc_first = kept([P, 2, P], U8, "h_sc_first%d" % half)
             quantize_h(h_w_first[:], h_sc_first[:], h_first[:])
             for t in range(4):
                 down_matmuls(
-                    first_banks[t // 2][:, t % 2, P * half : P * (half + 1)], t,
+                    first_planes[t][:, P * half : P * (half + 1)], t,
                     [h_w_first[:, a, :] for a in range(2)], [h_sc_first[:, a, :] for a in range(2)],
                 )
         first_y = [laid([P, 2, CH], F32, "first_y0", FIRST_Y_AT), kept([P, 2, CH], F32, "first_y1")]
         y[0] = [first_y[t // 2][:, t % 2, :] for t in range(4)]
-        for u in range(2):
-            nc.scalar.copy(first_y[u][:], first_banks[u][:])
+        for t in range(2):
+            nc.scalar.copy(y[0][t], first_planes[t])
+        nc.scalar.copy(first_y[1][:], first_high[:])
+
         for c in range(1, NCH):
-            h_in[c] = kept([P, 2, CH, 4], BF16, "h_in%d" % c)
+            h_in[c] = kept([P, 2, CH, 4], BF16, "h_in%d" % c, "h_w_first1" if c == 1 else None)
         gelu_pair(1, 0, 0, 0)
         gelu_pair(1, 0, 1, 1)
-        for t in range(4):
-            scale_plane(1, 0, t)
+        scale_planes(1, 0)
         gelu_pair(1, 1, 0, 4)
         weave_hidden(1, 0)
         gelu_pair(1, 1, 1, 5)
-        for t in range(4):
-            scale_plane(1, 1, t)
-        gather_words(2, 2, "wd_sc_raw")
+        scale_planes(1, 1)
+        gather_table(got_sc, tab_sc, LAST, 1, laid([P, CH], U8, "got_sc3", LATE_AT))
+        gather_table(got_w, tab_w, 2, 2, laid([P, 2 * CH], U32, "got_w2", LATE_AT + KIB))
         gelu_pair(2, 0, 0, 0)
         weave_hidden(1, 1)
         pages[1] = kept([P, T], F32, "page1", "tab_w")
@@ -260,7 +255,7 @@ def tile_list_modp_gelu_mix_resP_kernel(
             nc.vector.tensor_tensor(pages[t][:].indirect(picks(c)), total, wgo_sb[:, c * CH : (c + 1) * CH], MULT)
 
         def fresh_totals():
-            totals = ring.tile([P, 4, CH], F32, name="totals", tag="totals")
+            totals = ring.tile([P, 2, CH], F32, name="totals", tag="totals")
             return totals[:]
 
         out_planes = out_0.rearrange("(p t) c -> p t c", t=4)
@@ -274,14 +269,27 @@ def tile_list_modp_gelu_mix_resP_kernel(
                 nc.scalar.copy(pairs[:, 1, 0:SPLIT], pages[t][:, 0:SPLIT].unsqueeze(2).to_broadcast([P, SPLIT, 2]))
                 nc.scalar.copy(pairs[:, 1, SPLIT:T, 0], pages[t][:, SPLIT:T])
 
-        def pair_of_units(first, second, totals):
-            add_residual(*first, totals[:, 0, :])
-            add_residual(*second, totals[:, 1, :])
-            scatter(*first, totals[:, 0, :])
-            scatter(*second, totals[:, 1, :])
+        def two_planes(c, planes, totals):
+            for e, t in enumerate(planes):
+                add_residual(c, t, totals[:, e, :])
+            for e, t in enumerate(planes):
+                scatter(c, t, totals[:, e, :])
 
         def after_weave(c):
-            return kept([P, 2, CH], F32, "late%d" % c, "h_planes%d1" % c)
+            return kept([P, 2, CH], F32, "late%d" % c, "h_pairs%d1" % c)
+
+        def next_hidden(c, banks):
+            gelu_pair(c, 0, 1, 1)
+            scale_planes(c, 0)
+            gelu_pair(c, 1, 0, 2, high_pair(c - 1))
+            empty_low(c - 1, banks[0], "act%d01" % c)
+            weave_hidden(c, 0)
+            gelu_pair(c, 1, 1, 3)
+            scale_planes(c, 1)
+            nc.scalar.copy(high_pair(c - 1), banks[1][:])
+            if c < LAST:
+                gelu_pair(c + 1, 0, 0, 0)
+            weave_hidden(c, 1)
 
         totals = fresh_totals()
         for t in (0, 1):
@@ -290,29 +298,12 @@ def tile_list_modp_gelu_mix_resP_kernel(
         nc.gpsimd.memset(pages[2][:], 0.0)
         for t in (0, 1):
             scatter(0, t, totals[:, t, :])
-
-        def next_hidden(c, banks):
-            gelu_pair(c, 0, 1, 1)
-            for t in range(4):
-                scale_plane(c, 0, t)
-            gelu_pair(c, 1, 0, 2, high_pair(c - 1))
-            empty_low(c - 1, banks[0], "act%d01" % c)
-            weave_hidden(c, 0)
-            gelu_pair(c, 1, 1, 3)
-            for t in range(3):
-                scale_plane(c, 1, t)
-            nc.scalar.copy(high_pair(c - 1), banks[1][:])
-            scale_plane(c, 1, 3)
-            if c < LAST:
-                gelu_pair(c + 1, 0, 0, 0)
-            weave_hidden(c, 1)
-
         next_hidden(2, down(1))
-        pages[3] = kept([P, T], F32, "page3", "h_in1")
+        pages[3] = kept([P, T], F32, "page3", "h_w_first1")
         nc.gpsimd.memset(pages[3][:], 0.0)
-        pair_of_units((0, 2), (0, 3), after_weave(1))
+        two_planes(0, (2, 3), after_weave(1))
         for c in (1, 2):
-            pair_of_units((c, 0), (c, 1), fresh_totals())
+            two_planes(c, (0, 1), fresh_totals())
             banks = down(c + 1)
             if c + 1 < LAST:
                 next_hidden(c + 2, banks)
@@ -323,19 +314,19 @@ def tile_list_modp_gelu_mix_resP_kernel(
             add_residual(c, 2, late[:, 0, :])
             scatter(c, 2, late[:, 0, :])
         last = kept([P, 5 * CH], F32, "last")
-        totals = [last[:, (2 + t) * CH : (3 + t) * CH] for t in range(3)]
+        long_total = last[:, 0 : LAST * CH]
+        last_totals = [last[:, (2 + t) * CH : (3 + t) * CH] for t in range(3)]
         for t in (0, 1):
-            add_residual(LAST, t, totals[t])
-        scatter(LAST, 0, totals[0])
+            add_residual(LAST, t, last_totals[t])
+        scatter(LAST, 0, last_totals[0])
         finish_plane(0)
-        add_residual(LAST, 2, totals[2])
-        scatter(LAST, 1, totals[1])
+        add_residual(LAST, 2, last_totals[2])
+        scatter(LAST, 1, last_totals[1])
         finish_plane(1)
-        later = offsets[:, CH // 16 : J // 16]
-        nc.vector.tensor_tensor(last[:, 0 : LAST * CH], res[3][:].indirect(later), y_high[:, 1, :], ADD)
-        scatter(LAST, 2, totals[2])
+        nc.vector.tensor_tensor(long_total, res[3][:].indirect(picks(1, LAST)), y_high[:, 1, :], ADD)
+        scatter(LAST, 2, last_totals[2])
         finish_plane(2)
-        nc.vector.tensor_tensor(pages[3][:].indirect(later), last[:, 0 : LAST * CH], wgo_sb[:, CH:J], MULT)
+        nc.vector.tensor_tensor(pages[3][:].indirect(picks(1, LAST)), long_total, wgo_sb[:, CH:J], MULT)
         finish_plane(3)
 
         out_w = kept([P, T], U32, "out_w")
@@ -344,44 +335,36 @@ def tile_list_modp_gelu_mix_resP_kernel(
         pair_words = pairs[:].rearrange("p u c e -> p u (c e)").bitcast(F32)
         woven = {}
 
-        def woven_words(lo, hi):
+        def round_last_plane(copy, lo, hi):
+            copy(pairs[:, 1, lo:hi, 1], pages[3][:, lo:hi])
+
+        def weave_out(copy, lo, hi):
             woven[lo] = kept([P, hi - lo, 4], BF16, "woven%d" % lo)
-            return woven[lo][:].rearrange("p c t -> p (c t)").bitcast(F32).rearrange("p (c u) -> p c u", u=2)
-
-        def vector_piece(lo, hi):
-            nc.vector.tensor_copy(woven_words(lo, hi), pair_words[:, :, lo:hi].rearrange("p u c -> p c u"))
-
-        def scalar_round(lo, hi):
-            nc.scalar.copy(pairs[:, 1, lo:hi, 1], pages[3][:, lo:hi])
-
-        def scalar_weave(lo, hi):
-            nc.scalar.copy(woven_words(lo, hi), pair_words[:, :, lo:hi].rearrange("p u c -> p c u"))
+            words = woven[lo][:].rearrange("p c t -> p (c t)").bitcast(F32).rearrange("p (c u) -> p c u", u=2)
+            copy(words, pair_words[:, :, lo:hi].rearrange("p u c -> p c u"))
 
         def quantize_out(lo, hi):
             side = lo // (T // 2)
             nc.vector.quantize_mx(
                 out=out_w[:, lo:hi].bitcast(E4M3),
-                scales=out_sc[4 * side : P, lo - side * T // 2 : hi - side * T // 2],
+                scales=out_sc[UPPER_ROW * side : P, lo - side * T // 2 : hi - side * T // 2],
                 in_=woven[lo][:].rearrange("p c t -> p (c t)"),
             )
 
-        def store_codes(lo, hi):
+        vector_pieces = ((0, 512), (512, SPLIT))
+        scalar_pieces = ((SPLIT, 1536), (1536, 1792), (1792, T))
+        for piece in vector_pieces:
+            round_last_plane(nc.vector.tensor_copy, *piece)
+        round_last_plane(nc.scalar.copy, SPLIT, 1536)
+        round_last_plane(nc.scalar.copy, 1536, T)
+        for piece in scalar_pieces:
+            weave_out(nc.scalar.copy, *piece)
+        for piece in vector_pieces:
+            weave_out(nc.vector.tensor_copy, *piece)
+        for lo, hi in vector_pieces + scalar_pieces:
+            quantize_out(lo, hi)
             nc.sync.dma_start(out_words[:, lo:hi], out_w[:, lo:hi].bitcast(I32))
-
-        v0, v1 = (0, 512), (512, SPLIT)
-        s0, s1, s2 = (SPLIT, 1536), (1536, 1792), (1792, T)
-        for lo, hi in (v0, v1):
-            nc.vector.tensor_copy(pairs[:, 1, lo:hi, 1], pages[3][:, lo:hi])
-        scalar_round(*s0)
-        scalar_round(s1[0], s2[1])
-        for piece in (s0, s1, s2):
-            scalar_weave(*piece)
-        vector_piece(*v0)
-        vector_piece(*v1)
-        for piece in (v0, v1, s0, s1, s2):
-            quantize_out(*piece)
-            store_codes(*piece)
         for q in range(4):
             queue = nc.scalar if q < 3 else nc.sync
             rows = out_2[0, 4 * q : 4 * q + 4, :].bitcast(I32).rearrange("r (side c) -> side r c", side=2)
-            queue.dma_start(rows, out_sc[32 * q : 32 * q + 8, :].bitcast(I32))
+            queue.dma_start(rows, out_sc[32 * q : 32 * q + 2 * UPPER_ROW, :].bitcast(I32))

@@ -241,8 +241,8 @@ def tile_list_modp_gelu_mix_resP_kernel(
         weave_hidden(1, 0)
         gelu_pair(1, 1, 1, 5)
         scale_planes(1, 1)
-        gather_table(got_sc, tab_sc, LAST, 1, laid([P, CH], U8, "got_sc3", LATE_AT))
         gather_table(got_w, tab_w, 2, 2, laid([P, 2 * CH], U32, "got_w2", LATE_AT + KIB))
+        gather_table(got_sc, tab_sc, LAST, 1, laid([P, CH], U8, "got_sc3", LATE_AT))
         gelu_pair(2, 0, 0, 0)
         weave_hidden(1, 1)
         pages[1] = kept([P, T], F32, "page1", "tab_w")

@@ -25,11 +25,6 @@ NCH = J // CH
 LAST = NCH - 1
 UPPER_ROW = 4
 SCALE_ORDER = (0, 2, 1, 3)
-KIB = 1024
-PAGE2_AT = 0
-FIRST_Y_AT = 7 * KIB
-WD_AT = 16 * KIB
-LATE_AT = 19 * KIB
 SPLIT = T // 2
 
 
@@ -61,45 +56,50 @@ def tile_list_modp_gelu_mix_resP_kernel(
 
         tab_sc = kept([P, T], U8, "tab_sc")
         wu_sc_raw = kept([P, R], U8, "wu_sc_raw")
-        wd_sc_raw = laid([P, N], U8, "wd_sc_raw", LATE_AT)
+        wd_sc_raw = kept([P, N], U8, "wd_sc_raw")
         nc.gpsimd.memset(tab_sc[:].bitcast(I32), 0)
+        nc.gpsimd.memset(wu_sc_raw[:].bitcast(I32), 0)
         nc.vector.memset(wd_sc_raw[:].bitcast(I32), 0)
-        nc.vector.memset(wu_sc_raw[:].bitcast(I32), 0)
         pages = {0: kept([P, T], F32, "page0")}
         nc.vector.memset(pages[0][:], 0.0)
 
-        def load_scale_rows(tile, first, rows):
-            for q in range(4):
-                nc.sync.dma_start(
+        def load_scale_rows(tile, first, rows, quadrants=range(4), queue=nc.sync):
+            for q in quadrants:
+                queue.dma_start(
                     tile[32 * q + first : 32 * q + first + 4, :].bitcast(I32), rows[4 * q : 4 * q + 4, :].bitcast(I32)
                 )
 
         tab_w = kept([P, T], U32, "tab_w")
         wu_raw = kept([P, 2 * R], U8, "wu_raw")
-        wd8_raw = laid([P, N], I32, "wd8_raw", WD_AT + KIB)
-        wd4_raw = laid([P, 2 * N], U8, "wd4_raw", WD_AT)
+        wd8_raw = kept([P, N], I32, "wd8_raw")
+        wd4_raw = kept([P, 2 * N], U8, "wd4_raw")
         sm_sb = kept([P, 2, 4], F32, "sm_sb")
-        wgo_sb = kept([P, J], F32, "wgo_sb")
+        wgo_first = kept([P, CH], F32, "wgo_first")
+        wgo_rest = kept([P, J - CH], F32, "wgo_rest")
         res = [kept([P, T], F32, "res%d" % t) for t in range(4)]
         rT_planes = rT.rearrange("(p t) c -> p t c", t=4)
         nc.gpsimd.dma_start(sm_sb[:], sm.rearrange("(a p t) -> p a t", a=2, t=4))
         nc.sync.dma_start(offsets[:], offs)
         nc.sync.dma_start(wu_raw[:].bitcast(I32), wu_words[0].bitcast(I32))
         load_scale_rows(tab_sc, 0, tab_scales[0])
+        load_scale_rows(wu_sc_raw, 0, wu_scales[0], range(1))
         nc.sync.dma_start(tab_w[:].bitcast(I32), tab_words[0].rearrange("p t i -> p (t i)").bitcast(I32))
-        load_scale_rows(wu_sc_raw, 0, wu_scales[0])
+        load_scale_rows(wu_sc_raw, 0, wu_scales[0], range(1, 4))
         nc.sync.dma_start(wd8_raw[:], wd8_words[0].rearrange("p n i -> p (n i)").bitcast(I32))
         nc.sync.dma_start(wd4_raw[:].bitcast(I32), wd4_words[0].bitcast(I32))
         load_scale_rows(wd_sc_raw, 0, wd4_scales[0])
         load_scale_rows(wd_sc_raw, UPPER_ROW, wd8_scales[0])
         nc.sync.dma_start(res[0][:], rT_planes[:, 0, :])
-        nc.sync.dma_start(res[1][:], rT_planes[:, 1, :])
-        nc.sync.dma_start(wgo_sb[:], wgo)
-        for t in (2, 3):
+        nc.sync.dma_start(wgo_first[:], wgo[:, 0:CH])
+        for t in (1, 2, 3):
             nc.sync.dma_start(res[t][:], rT_planes[:, t, :])
+        nc.sync.dma_start(wgo_rest[:], wgo[:, CH:J])
 
-        def deal(dst, src):
-            nc.vector.tensor_copy(dst.rearrange("p (t m) -> p t m", t=4), src.rearrange("p (m t) -> p t m", t=4))
+        def weights_of(first, chunks=1):
+            return wgo_first[:] if first == 0 else wgo_rest[:, (first - 1) * CH : (first - 1 + chunks) * CH]
+
+        def deal(dst, src, engine=nc.gpsimd):
+            engine.tensor_copy(dst.rearrange("p (t m) -> p t m", t=4), src.rearrange("p (m t) -> p t m", t=4))
 
         got_sc = {}
         got_w = {}
@@ -109,12 +109,12 @@ def tile_list_modp_gelu_mix_resP_kernel(
             for c in range(chunks):
                 got[first + c] = tile[:, c * CH : (c + 1) * CH]
 
-        wu = kept([P, 2 * R], U8, "wu")
+        wu = [kept([P, 2 * PASS], U8, "wu%d" % a) for a in range(2)]
         wu_sc = [kept([P, PASS], U8, "wu_sc%d" % a) for a in range(2)]
 
         def up_matmul(out, c, a, t, cols):
             nc.tensor.matmul_mx(
-                out, lhsT=wu[:, 2 * P * (4 * a + t) : 2 * P * (4 * a + t + 1)].bitcast(E2M1),
+                out, lhsT=wu[a][:, 2 * P * t : 2 * P * (t + 1)].bitcast(E2M1),
                 lhsT_scale=wu_sc[a][:, P * t : P * (t + 1)],
                 rhs=got_w[c][:, cols].bitcast(E4M3), rhs_scale=got_sc[c][:, cols],
                 start=True, stop=True,
@@ -142,11 +142,11 @@ def tile_list_modp_gelu_mix_resP_kernel(
         h_in = {}
         y = {}
 
-        def gelu_pair(c, a, u, b, act=None):
+        def gelu_pair(c, a, u, b, on=None):
             bank = bank_tile([P, 2, CH], b)
             for e in range(2):
                 up_matmul(bank[:, e, :], c, a, 2 * u + e, slice(0, CH))
-            acts[c, a, u] = act if act is not None else kept([P, 2, CH], F32, "act%d%d%d" % (c, a, u))[:]
+            acts[c, a, u] = kept([P, 2, CH], F32, "act%d%d%d" % (c, a, u), on)[:]
             nc.scalar.activation(acts[c, a, u], bank[:], GELU)
 
         def scale_planes(c, a):
@@ -171,11 +171,14 @@ def tile_list_modp_gelu_mix_resP_kernel(
                 h_pairs[c, a][:].rearrange("p u j e -> p u (j e)").bitcast(F32).rearrange("p u j -> p j u"),
             )
 
-        def down(c):
-            h_w = ring.tile([P, 2, CH], U32, name="h_w", tag="h_w", align_bytes=64)
+        h_w_tag = {}
+
+        def down(c, after):
+            h_w_tag[c] = after or "h_w%d" % c
+            h_w = kept([P, 2, CH], U32, "h_w%d" % c, after)
             h_sc = ring.tile([P, 2, CH], U8, name="h_sc", tag="h_sc", align_bytes=64)
             quantize_h(h_w[:], h_sc[:], h_in[c][:])
-            banks = [bank_tile([P, 2, CH], 4 + 2 * (c % 2) + u) for u in range(2)]
+            banks = [bank_tile([P, 2, CH], 6 + u) for u in range(2)]
             for t in range(4):
                 for half in range(2):
                     cols = slice(P * half, P * (half + 1))
@@ -185,12 +188,11 @@ def tile_list_modp_gelu_mix_resP_kernel(
                     )
             return banks
 
-        nc.vector.tensor_copy(
-            wu[:].bitcast(U16).rearrange("p (a t m) -> p a t m", a=2, t=4),
-            wu_raw[:].bitcast(U16).rearrange("p (a m t) -> p a t m", a=2, t=4),
-        )
-        gather_table(got_sc, tab_sc, 0, LAST, kept([P, LAST * CH], U8, "got_sc0"))
+        gather_table(got_sc, tab_sc, 0, NCH, kept([P, J], U8, "got_sc0"))
         gather_table(got_w, tab_w, 0, 1, kept([P, CH], U32, "got_w0"))
+        for a in range(2):
+            deal(wu[a][:].bitcast(U16), wu_raw[:].bitcast(U16)[:, PASS * a : PASS * (a + 1)])
+        gather_table(got_w, tab_w, 1, LAST, kept([P, LAST * CH], U32, "got_w1"))
         for a in range(2):
             deal(wu_sc[a][:], wu_sc_raw[:, PASS * a : PASS * (a + 1)])
         act_first = {}
@@ -203,21 +205,19 @@ def tile_list_modp_gelu_mix_resP_kernel(
                 nc.scalar.activation(act_first[half, a][:], bank[:].rearrange("p t j -> p j t"), GELU)
         wd8 = kept([P, N], I32, "wd8")
         wd4 = kept([P, 2 * N], U8, "wd4")
-        nc.vector.tensor_copy(
+        nc.gpsimd.tensor_copy(
             wd8[:].rearrange("p (t m i) -> p m t i", t=4, i=4), wd8_raw[:].rearrange("p (m i t) -> p m t i", t=4, i=4)
         )
         deal(wd4[:].bitcast(U16), wd4_raw[:].bitcast(U16))
-        gather_table(got_w, tab_w, 1, 1, kept([P, CH], U32, "got_w1", "wu_sc_raw"))
+        wd_sc = kept([P, N], U8, "wd_sc")
+        deal(wd_sc[:], wd_sc_raw[:])
         first_high = bank_tile([P, 2, CH], 5)
         first_planes = [bank_tile([P, CH], 6)[:], bank_tile([P, CH], 4)[:], first_high[:, 0, :], first_high[:, 1, :]]
         for half in range(2):
-            h_first = laid([P, 2, P, 4], BF16, "h_first%d" % half, (WD_AT, LATE_AT)[half])
+            h_first = laid([P, 2, P, 4], BF16, "h_first%d" % half, (9 * 1024, 7 * 1024)[half])
             for a in range(2):
                 factors = sm_sb[:, a, :].unsqueeze(1).to_broadcast([P, P, 4])
                 nc.vector.tensor_tensor(h_first[:, a], act_first[half, a][:], factors, MULT)
-            if half == 0:
-                wd_sc = kept([P, N], U8, "wd_sc", "act_first00")
-                deal(wd_sc[:], wd_sc_raw[:])
             h_w_first = kept([P, 2, P], U32, "h_w_first%d" % half)
             h_sc_first = kept([P, 2, P], U8, "h_sc_first%d" % half)
             quantize_h(h_w_first[:], h_sc_first[:], h_first[:])
@@ -226,14 +226,14 @@ def tile_list_modp_gelu_mix_resP_kernel(
                     first_planes[t][:, P * half : P * (half + 1)], t,
                     [h_w_first[:, a, :] for a in range(2)], [h_sc_first[:, a, :] for a in range(2)],
                 )
-        first_y = [laid([P, 2, CH], F32, "first_y0", FIRST_Y_AT), kept([P, 2, CH], F32, "first_y1")]
+        first_y = [kept([P, 2, CH], F32, "first_y0"), kept([P, 2, CH], F32, "first_y1")]
         y[0] = [first_y[t // 2][:, t % 2, :] for t in range(4)]
-        for t in range(2):
-            nc.scalar.copy(y[0][t], first_planes[t])
+        first_res = laid([P, CH], F32, "first_res", 8 * 1024)
+        nc.vector.tensor_copy(first_res[:], res[0][:].indirect(picks(0)))
+        nc.scalar.copy(y[0][1], first_planes[1])
         nc.scalar.copy(first_y[1][:], first_high[:])
 
-        for c in range(1, NCH):
-            h_in[c] = kept([P, 2, CH, 4], BF16, "h_in%d" % c, "h_w_first1" if c == 1 else None)
+        h_in[1] = kept([P, 2, CH, 4], BF16, "h_in1")
         gelu_pair(1, 0, 0, 0)
         gelu_pair(1, 0, 1, 1)
         scale_planes(1, 0)
@@ -241,21 +241,25 @@ def tile_list_modp_gelu_mix_resP_kernel(
         weave_hidden(1, 0)
         gelu_pair(1, 1, 1, 5)
         scale_planes(1, 1)
-        gather_table(got_w, tab_w, 2, 2, laid([P, 2 * CH], U32, "got_w2", LATE_AT + KIB))
-        gather_table(got_sc, tab_sc, LAST, 1, laid([P, CH], U8, "got_sc3", LATE_AT))
-        gelu_pair(2, 0, 0, 0)
+        gelu_pair(2, 0, 0, 0, "act110")
         weave_hidden(1, 1)
-        pages[1] = kept([P, T], F32, "page1", "tab_w")
-        nc.gpsimd.memset(pages[1][:], 0.0)
+        pages[1] = laid([P, T], F32, "page1", 0)
+        pages[2] = kept([P, T], F32, "page2", "h_w_first1")
+        pages[3] = kept([P, T], F32, "page3", "h_sc_first1")
+        for t in (1, 2, 3):
+            nc.gpsimd.memset(pages[t][:], 0.0)
 
         def add_residual(c, t, total):
-            nc.vector.tensor_tensor(total, res[t][:].indirect(picks(c)), y[c][t], ADD)
+            if (c, t) == (0, 0):
+                nc.vector.tensor_tensor(total, first_planes[0], first_res[:], ADD)
+            else:
+                nc.vector.tensor_tensor(total, res[t][:].indirect(picks(c)), y[c][t], ADD)
 
         def scatter(c, t, total):
-            nc.vector.tensor_tensor(pages[t][:].indirect(picks(c)), total, wgo_sb[:, c * CH : (c + 1) * CH], MULT)
+            nc.vector.tensor_tensor(pages[t][:].indirect(picks(c)), total, weights_of(c), MULT)
 
         def fresh_totals():
-            totals = ring.tile([P, 2, CH], F32, name="totals", tag="totals")
+            totals = ring.tile([P, 3, CH], F32, name="totals", tag="totals")
             return totals[:]
 
         out_planes = out_0.rearrange("(p t) c -> p t c", t=4)
@@ -269,50 +273,43 @@ def tile_list_modp_gelu_mix_resP_kernel(
                 nc.scalar.copy(pairs[:, 1, 0:SPLIT], pages[t][:, 0:SPLIT].unsqueeze(2).to_broadcast([P, SPLIT, 2]))
                 nc.scalar.copy(pairs[:, 1, SPLIT:T, 0], pages[t][:, SPLIT:T])
 
-        def two_planes(c, planes, totals):
-            for e, t in enumerate(planes):
-                add_residual(c, t, totals[:, e, :])
-            for e, t in enumerate(planes):
-                scatter(c, t, totals[:, e, :])
+        def first_planes_of(c, count):
+            totals = [kept([P, CH], F32, "total%d%d" % (c, t), "h_pairs11" if (c, t) == (1, 0) else None) for t in range(count)]
+            add_residual(c, 0, totals[0][:])
+            for t in range(count):
+                if t < count - 1:
+                    add_residual(c, t + 1, totals[t + 1][:])
+                scatter(c, t, totals[t][:])
 
         def after_weave(c):
             return kept([P, 2, CH], F32, "late%d" % c, "h_pairs%d1" % c)
 
         def next_hidden(c, banks):
-            gelu_pair(c, 0, 1, 1)
+            gelu_pair(c, 0, 1, 1, "act%d11" % (c - 1))
             scale_planes(c, 0)
-            gelu_pair(c, 1, 0, 2, high_pair(c - 1))
-            empty_low(c - 1, banks[0], "act%d01" % c)
-            weave_hidden(c, 0)
-            gelu_pair(c, 1, 1, 3)
-            scale_planes(c, 1)
+            gelu_pair(c, 1, 0, 2, None if c < LAST else "h_pairs%d0" % (c - 1))
+            empty_low(c - 1, banks[0], None)
             nc.scalar.copy(high_pair(c - 1), banks[1][:])
+            h_in[c] = kept([P, 2, CH, 4], BF16, "h_in%d" % c, h_w_tag[c - 1])
+            weave_hidden(c, 0)
+            gelu_pair(c, 1, 1, 6)
+            scale_planes(c, 1)
             if c < LAST:
-                gelu_pair(c + 1, 0, 0, 0)
+                gelu_pair(c + 1, 0, 0, 0, "act%d10" % c)
             weave_hidden(c, 1)
 
-        totals = fresh_totals()
-        for t in (0, 1):
-            add_residual(0, t, totals[:, t, :])
-        pages[2] = laid([P, T], F32, "page2", PAGE2_AT)
-        nc.gpsimd.memset(pages[2][:], 0.0)
-        for t in (0, 1):
-            scatter(0, t, totals[:, t, :])
-        next_hidden(2, down(1))
-        pages[3] = kept([P, T], F32, "page3", "h_w_first1")
-        nc.gpsimd.memset(pages[3][:], 0.0)
-        two_planes(0, (2, 3), after_weave(1))
-        for c in (1, 2):
-            two_planes(c, (0, 1), fresh_totals())
-            banks = down(c + 1)
+        for c in range(LAST):
+            before = 3 if c == 0 else 2
+            first_planes_of(c, before)
+            banks = down(c + 1, "total02" if c == 0 else None)
             if c + 1 < LAST:
                 next_hidden(c + 2, banks)
             else:
                 empty_low(LAST, banks[0], None)
                 nc.scalar.copy(high_pair(LAST), banks[1][:])
             late = after_weave(c + 1)
-            add_residual(c, 2, late[:, 0, :])
-            scatter(c, 2, late[:, 0, :])
+            add_residual(c, before, late[:, 0, :])
+            scatter(c, before, late[:, 0, :])
         last = kept([P, 5 * CH], F32, "last")
         long_total = last[:, 0 : LAST * CH]
         last_totals = [last[:, (2 + t) * CH : (3 + t) * CH] for t in range(3)]
@@ -326,7 +323,7 @@ def tile_list_modp_gelu_mix_resP_kernel(
         nc.vector.tensor_tensor(long_total, res[3][:].indirect(picks(1, LAST)), y_high[:, 1, :], ADD)
         scatter(LAST, 2, last_totals[2])
         finish_plane(2)
-        nc.vector.tensor_tensor(pages[3][:].indirect(picks(1, LAST)), long_total, wgo_sb[:, CH:J], MULT)
+        nc.vector.tensor_tensor(pages[3][:].indirect(picks(1, LAST)), long_total, weights_of(1, LAST), MULT)
         finish_plane(3)
 
         out_w = kept([P, T], U32, "out_w")

@@ -196,10 +196,10 @@ def tile_list_modp_gelu_mix_resP_kernel(
         for a in range(2):
             deal(wu_sc[a][:], wu_sc_raw[:, PASS * a : PASS * (a + 1)])
         act_first = {}
-        for half in range(2):
-            for a in range(2):
+        for a in range(2):
+            for half in range(2):
                 act_first[half, a] = kept([P, P, 4], F32, "act_first%d%d" % (half, a))
-                bank = bank_tile([P, 4, P], 2 * half + a)
+                bank = bank_tile([P, 4, P], 2 * a + half)
                 for t in range(4):
                     up_matmul(bank[:, t, :], 0, a, t, slice(P * half, P * (half + 1)))
                 nc.scalar.activation(act_first[half, a][:], bank[:].rearrange("p t j -> p j t"), GELU)
@@ -213,18 +213,29 @@ def tile_list_modp_gelu_mix_resP_kernel(
         deal(wd_sc[:], wd_sc_raw[:])
         first_high = bank_tile([P, 2, CH], 5)
         first_planes = [bank_tile([P, CH], 6)[:], bank_tile([P, CH], 4)[:], first_high[:, 0, :], first_high[:, 1, :]]
-        for half in range(2):
-            h_first = laid([P, 2, P, 4], BF16, "h_first%d" % half, (9 * 1024, 7 * 1024)[half])
-            for a in range(2):
-                factors = sm_sb[:, a, :].unsqueeze(1).to_broadcast([P, P, 4])
-                nc.vector.tensor_tensor(h_first[:, a], act_first[half, a][:], factors, MULT)
-            h_w_first = kept([P, 2, P], U32, "h_w_first%d" % half)
-            h_sc_first = kept([P, 2, P], U8, "h_sc_first%d" % half)
-            quantize_h(h_w_first[:], h_sc_first[:], h_first[:])
-            for t in range(4):
+        h_first = [kept([P, 2, P, 4], BF16, "h_first0"), laid([P, 2, P, 4], BF16, "h_first1", 7 * 1024)]
+        h_w_first = [kept([P, 2, P], U32, "h_w_first%d" % a) for a in range(2)]
+        h_sc_first = [kept([P, 2, P], U8, "h_sc_first%d" % a) for a in range(2)]
+
+        def first_product(a, half):
+            factors = sm_sb[:, a, :].unsqueeze(1).to_broadcast([P, P, 4])
+            nc.vector.tensor_tensor(h_first[a][:, half], act_first[half, a][:], factors, MULT)
+
+        def first_quantize(a, halves):
+            quantize_h(h_w_first[a][:, halves], h_sc_first[a][:, halves], h_first[a][:, halves])
+
+        first_product(0, 0)
+        first_product(0, 1)
+        first_product(1, 0)
+        first_quantize(0, slice(0, 2))
+        first_product(1, 1)
+        first_quantize(1, slice(0, 1))
+        first_quantize(1, slice(1, 2))
+        for t in range(4):
+            for half in range(2):
                 down_matmuls(
                     first_planes[t][:, P * half : P * (half + 1)], t,
-                    [h_w_first[:, a, :] for a in range(2)], [h_sc_first[:, a, :] for a in range(2)],
+                    [h_w_first[a][:, half, :] for a in range(2)], [h_sc_first[a][:, half, :] for a in range(2)],
                 )
         first_y = [kept([P, 2, CH], F32, "first_y0"), kept([P, 2, CH], F32, "first_y1")]
         y[0] = [first_y[t // 2][:, t % 2, :] for t in range(4)]
@@ -274,7 +285,7 @@ def tile_list_modp_gelu_mix_resP_kernel(
                 nc.scalar.copy(pairs[:, 1, SPLIT:T, 0], pages[t][:, SPLIT:T])
 
         def first_planes_of(c, count):
-            totals = [kept([P, CH], F32, "total%d%d" % (c, t), "h_pairs11" if (c, t) == (1, 0) else None) for t in range(count)]
+            totals = [kept([P, CH], F32, "total%d%d" % (c, t), "first_y1" if (c, t) == (1, 0) else None) for t in range(count)]
             add_residual(c, 0, totals[0][:])
             for t in range(count):
                 if t < count - 1:

@@ -25,6 +25,10 @@ NCH = J // CH
 LAST = NCH - 1
 UPPER_ROW = 4
 SCALE_ORDER = (0, 2, 1, 3)
+KIB = 1024
+PAGE1_AT = 0
+H_FIRST_AT = 7 * KIB
+FIRST_RES_AT = 8 * KIB
 SPLIT = T // 2
 
 
@@ -63,9 +67,9 @@ def tile_list_modp_gelu_mix_resP_kernel(
         pages = {0: kept([P, T], F32, "page0")}
         nc.vector.memset(pages[0][:], 0.0)
 
-        def load_scale_rows(tile, first, rows, quadrants=range(4), queue=nc.sync):
+        def load_scale_rows(tile, first, rows, quadrants=range(4)):
             for q in quadrants:
-                queue.dma_start(
+                nc.sync.dma_start(
                     tile[32 * q + first : 32 * q + first + 4, :].bitcast(I32), rows[4 * q : 4 * q + 4, :].bitcast(I32)
                 )
 
@@ -98,8 +102,8 @@ def tile_list_modp_gelu_mix_resP_kernel(
         def weights_of(first, chunks=1):
             return wgo_first[:] if first == 0 else wgo_rest[:, (first - 1) * CH : (first - 1 + chunks) * CH]
 
-        def deal(dst, src, engine=nc.gpsimd):
-            engine.tensor_copy(dst.rearrange("p (t m) -> p t m", t=4), src.rearrange("p (m t) -> p t m", t=4))
+        def deal(dst, src):
+            nc.gpsimd.tensor_copy(dst.rearrange("p (t m) -> p t m", t=4), src.rearrange("p (m t) -> p t m", t=4))
 
         got_sc = {}
         got_w = {}
@@ -160,8 +164,8 @@ def tile_list_modp_gelu_mix_resP_kernel(
         def high_pair(c):
             return y_high[:, :, (c - 1) * CH : c * CH]
 
-        def empty_low(c, bank, on):
-            low = kept([P, 2, CH], F32, "y_low%d" % c, on)
+        def empty_low(c, bank):
+            low = kept([P, 2, CH], F32, "y_low%d" % c)
             nc.scalar.copy(low[:], bank[:])
             y[c] = [low[:, 0, :], low[:, 1, :], high_pair(c)[:, 0, :], high_pair(c)[:, 1, :]]
 
@@ -171,11 +175,11 @@ def tile_list_modp_gelu_mix_resP_kernel(
                 h_pairs[c, a][:].rearrange("p u j e -> p u (j e)").bitcast(F32).rearrange("p u j -> p j u"),
             )
 
-        h_w_tag = {}
+        def codes_place(c):
+            return "total02" if c == 1 else "h_w%d" % c
 
-        def down(c, after):
-            h_w_tag[c] = after or "h_w%d" % c
-            h_w = kept([P, 2, CH], U32, "h_w%d" % c, after)
+        def down(c):
+            h_w = kept([P, 2, CH], U32, "h_w%d" % c, codes_place(c))
             h_sc = ring.tile([P, 2, CH], U8, name="h_sc", tag="h_sc", align_bytes=64)
             quantize_h(h_w[:], h_sc[:], h_in[c][:])
             banks = [bank_tile([P, 2, CH], 6 + u) for u in range(2)]
@@ -213,7 +217,7 @@ def tile_list_modp_gelu_mix_resP_kernel(
         deal(wd_sc[:], wd_sc_raw[:])
         first_high = bank_tile([P, 2, CH], 5)
         first_planes = [bank_tile([P, CH], 6)[:], bank_tile([P, CH], 4)[:], first_high[:, 0, :], first_high[:, 1, :]]
-        h_first = [kept([P, 2, P, 4], BF16, "h_first0"), laid([P, 2, P, 4], BF16, "h_first1", 7 * 1024)]
+        h_first = [kept([P, 2, P, 4], BF16, "h_first0"), laid([P, 2, P, 4], BF16, "h_first1", H_FIRST_AT)]
         h_w_first = [kept([P, 2, P], U32, "h_w_first%d" % a) for a in range(2)]
         h_sc_first = [kept([P, 2, P], U8, "h_sc_first%d" % a) for a in range(2)]
 
@@ -237,12 +241,13 @@ def tile_list_modp_gelu_mix_resP_kernel(
                     first_planes[t][:, P * half : P * (half + 1)], t,
                     [h_w_first[a][:, half, :] for a in range(2)], [h_sc_first[a][:, half, :] for a in range(2)],
                 )
-        first_y = [kept([P, 2, CH], F32, "first_y0"), kept([P, 2, CH], F32, "first_y1")]
-        y[0] = [first_y[t // 2][:, t % 2, :] for t in range(4)]
-        first_res = laid([P, CH], F32, "first_res", 8 * 1024)
+        first_res = laid([P, CH], F32, "first_res", FIRST_RES_AT)
         nc.vector.tensor_copy(first_res[:], res[0][:].indirect(picks(0)))
-        nc.scalar.copy(y[0][1], first_planes[1])
-        nc.scalar.copy(first_y[1][:], first_high[:])
+        first_y1 = kept([P, CH], F32, "first_y1")
+        first_y_high = kept([P, 2, CH], F32, "first_y_high")
+        y[0] = {1: first_y1[:], 2: first_y_high[:, 0, :], 3: first_y_high[:, 1, :]}
+        nc.scalar.copy(first_y1[:], first_planes[1])
+        nc.scalar.copy(first_y_high[:], first_high[:])
 
         h_in[1] = kept([P, 2, CH, 4], BF16, "h_in1")
         gelu_pair(1, 0, 0, 0)
@@ -254,7 +259,7 @@ def tile_list_modp_gelu_mix_resP_kernel(
         scale_planes(1, 1)
         gelu_pair(2, 0, 0, 0, "act110")
         weave_hidden(1, 1)
-        pages[1] = laid([P, T], F32, "page1", 0)
+        pages[1] = laid([P, T], F32, "page1", PAGE1_AT)
         pages[2] = kept([P, T], F32, "page2", "h_w_first1")
         pages[3] = kept([P, T], F32, "page3", "h_sc_first1")
         for t in (1, 2, 3):
@@ -269,10 +274,6 @@ def tile_list_modp_gelu_mix_resP_kernel(
         def scatter(c, t, total):
             nc.vector.tensor_tensor(pages[t][:].indirect(picks(c)), total, weights_of(c), MULT)
 
-        def fresh_totals():
-            totals = ring.tile([P, 3, CH], F32, name="totals", tag="totals")
-            return totals[:]
-
         out_planes = out_0.rearrange("(p t) c -> p t c", t=4)
         pairs = kept([P, 2, T, 2], BF16, "pairs")
 
@@ -285,7 +286,10 @@ def tile_list_modp_gelu_mix_resP_kernel(
                 nc.scalar.copy(pairs[:, 1, SPLIT:T, 0], pages[t][:, SPLIT:T])
 
         def first_planes_of(c, count):
-            totals = [kept([P, CH], F32, "total%d%d" % (c, t), "first_y1" if (c, t) == (1, 0) else None) for t in range(count)]
+            totals = [
+                kept([P, CH], F32, "total%d%d" % (c, t), "first_y_high" if (c, t) == (1, 0) else None)
+                for t in range(count)
+            ]
             add_residual(c, 0, totals[0][:])
             for t in range(count):
                 if t < count - 1:
@@ -293,15 +297,15 @@ def tile_list_modp_gelu_mix_resP_kernel(
                 scatter(c, t, totals[t][:])
 
         def after_weave(c):
-            return kept([P, 2, CH], F32, "late%d" % c, "h_pairs%d1" % c)
+            return kept([P, CH], F32, "late%d" % c, "h_pairs%d1" % c)
 
         def next_hidden(c, banks):
             gelu_pair(c, 0, 1, 1, "act%d11" % (c - 1))
             scale_planes(c, 0)
             gelu_pair(c, 1, 0, 2, None if c < LAST else "h_pairs%d0" % (c - 1))
-            empty_low(c - 1, banks[0], None)
+            empty_low(c - 1, banks[0])
             nc.scalar.copy(high_pair(c - 1), banks[1][:])
-            h_in[c] = kept([P, 2, CH, 4], BF16, "h_in%d" % c, h_w_tag[c - 1])
+            h_in[c] = kept([P, 2, CH, 4], BF16, "h_in%d" % c, codes_place(c - 1))
             weave_hidden(c, 0)
             gelu_pair(c, 1, 1, 6)
             scale_planes(c, 1)
@@ -312,15 +316,15 @@ def tile_list_modp_gelu_mix_resP_kernel(
         for c in range(LAST):
             before = 3 if c == 0 else 2
             first_planes_of(c, before)
-            banks = down(c + 1, "total02" if c == 0 else None)
+            banks = down(c + 1)
             if c + 1 < LAST:
                 next_hidden(c + 2, banks)
             else:
-                empty_low(LAST, banks[0], None)
+                empty_low(LAST, banks[0])
                 nc.scalar.copy(high_pair(LAST), banks[1][:])
             late = after_weave(c + 1)
-            add_residual(c, before, late[:, 0, :])
-            scatter(c, before, late[:, 0, :])
+            add_residual(c, before, late[:])
+            scatter(c, before, late[:])
         last = kept([P, 5 * CH], F32, "last")
         long_total = last[:, 0 : LAST * CH]
         last_totals = [last[:, (2 + t) * CH : (3 + t) * CH] for t in range(3)]

from contextlib import ExitStack

import concourse.mybir as mybir

K, R, N, T, J = 512, 1024, 512, 2048, 1024
FLOPS = 2 * K * R * J + 2 * R * N * J

F32 = mybir.dt.float32
BF16 = mybir.dt.bfloat16
I32 = mybir.dt.int32
U32 = mybir.dt.uint32
U16 = mybir.dt.uint16
U8 = mybir.dt.uint8
E4M3 = mybir.dt.float8_e4m3fn_x4
E2M1 = mybir.dt.float4_e2m1fn_x4
GELU = mybir.ActivationFunctionType.Gelu_apprx_tanh
COPY = mybir.ActivationFunctionType.Copy
MULT = mybir.AluOpType.mult
ADD = mybir.AluOpType.add

P = 128
PASS = 512
CH = 256
NCH = J // CH
LAST = NCH - 1
UPPER_ROW = 4
SCALE_ORDER = (0, 2, 1, 3)
KIB = 1024
PAGE1_AT = 0
H_FIRST_AT = 7 * KIB
FIRST_RES_AT = 8 * KIB
SPLIT = T // 2


def tile_list_modp_gelu_mix_resP_kernel(
    tc, tab_words, tab_scales, wu_words, wu_scales, sm, wd8_words, wd8_scales, wd4_words, wd4_scales,
    rT, wgo, offs, out_0, out_1, out_2
):
    nc = tc.nc
    with ExitStack() as ctx:
        lists = ctx.enter_context(tc.tile_pool(name="lists", bufs=1))
        keep = ctx.enter_context(tc.tile_pool(name="keep", bufs=1))
        ring = ctx.enter_context(tc.tile_pool(name="ring", bufs=2))
        placed = ctx.enter_context(tc.tile_pool(name="placed", bufs=1))
        psum = ctx.enter_context(tc.psum_pool(name="psum", bufs=1))

        def kept(shape, dtype, name, on=None):
            return keep.tile(shape, dtype, name=name, tag=on or name, align_bytes=64)

        def laid(shape, dtype, name, offset):
            return placed.tile(shape, dtype, name=name, tag=name, align_bytes=64, offset=offset)

        def bank_tile(shape, b):
            return psum.tile(shape, F32, name="bank%d" % b, tag="bank%d" % b)

        offsets = lists.tile([P, J // 16], U16, name="offsets")

        def picks(first, chunks=1):
            return offsets[:, first * CH // 16 : (first + chunks) * CH // 16]

        tab_sc = kept([P, T], U8, "tab_sc")
        wu_sc_raw = kept([P, R], U8, "wu_sc_raw")
        wd_sc_raw = kept([P, N], U8, "wd_sc_raw")
        nc.gpsimd.memset(tab_sc[:].bitcast(I32), 0)
        nc.gpsimd.memset(wu_sc_raw[:].bitcast(I32), 0)
        nc.vector.memset(wd_sc_raw[:].bitcast(I32), 0)
        pages = {0: kept([P, T], F32, "page0")}
        nc.vector.memset(pages[0][:], 0.0)

        def load_scale_rows(tile, first, rows, quadrants=range(4)):
            for q in quadrants:
                nc.sync.dma_start(
                    tile[32 * q + first : 32 * q + first + 4, :].bitcast(I32), rows[4 * q : 4 * q + 4, :].bitcast(I32)
                )

        tab_w = kept([P, T], U32, "tab_w")
        wu_raw = kept([P, 2 * R], U8, "wu_raw")
        wd8_raw = kept([P, N], I32, "wd8_raw")
        wd4_raw = kept([P, 2 * N], U8, "wd4_raw")
        sm_sb = kept([P, 2, 4], F32, "sm_sb")
        wgo_first = kept([P, CH], F32, "wgo_first")
        wgo_rest = kept([P, J - CH], F32, "wgo_rest")
        res = [kept([P, T], F32, "res%d" % t) for t in range(4)]
        rT_planes = rT.rearrange("(p t) c -> p t c", t=4)
        nc.gpsimd.dma_start(sm_sb[:], sm.rearrange("(a p t) -> p a t", a=2, t=4))
        nc.sync.dma_start(offsets[:], offs)
        nc.sync.dma_start(wu_raw[:].bitcast(I32), wu_words[0].bitcast(I32))
        load_scale_rows(tab_sc, 0, tab_scales[0])
        load_scale_rows(wu_sc_raw, 0, wu_scales[0], range(1))
        nc.sync.dma_start(tab_w[:].bitcast(I32), tab_words[0].rearrange("p t i -> p (t i)").bitcast(I32))
        load_scale_rows(wu_sc_raw, 0, wu_scales[0], range(1, 4))
        nc.sync.dma_start(wd8_raw[:], wd8_words[0].rearrange("p n i -> p (n i)").bitcast(I32))
        nc.sync.dma_start(wd4_raw[:].bitcast(I32), wd4_words[0].bitcast(I32))
        load_scale_rows(wd_sc_raw, 0, wd4_scales[0])
        load_scale_rows(wd_sc_raw, UPPER_ROW, wd8_scales[0])
        nc.sync.dma_start(res[0][:], rT_planes[:, 0, :])
        nc.sync.dma_start(wgo_first[:], wgo[:, 0:CH])
        for t in (1, 2, 3):
            nc.sync.dma_start(res[t][:], rT_planes[:, t, :])
        nc.sync.dma_start(wgo_rest[:], wgo[:, CH:J])

        def weights_of(first, chunks=1):
            return wgo_first[:] if first == 0 else wgo_rest[:, (first - 1) * CH : (first - 1 + chunks) * CH]

        def deal(dst, src):
            nc.gpsimd.tensor_copy(dst.rearrange("p (t m) -> p t m", t=4), src.rearrange("p (m t) -> p t m", t=4))

        got_sc = {}
        got_w = {}

        def gather_table(got, table, first, chunks, tile):
            nc.vector.tensor_copy(tile[:], table[:].indirect(picks(first, chunks)))
            for c in range(chunks):
                got[first + c] = tile[:, c * CH : (c + 1) * CH]

        wu = [kept([P, 2 * PASS], U8, "wu%d" % a) for a in range(2)]
        wu_sc = [kept([P, PASS], U8, "wu_sc%d" % a) for a in range(2)]

        def up_matmul(out, c, a, t, cols):
            nc.tensor.matmul_mx(
                out, lhsT=wu[a][:, 2 * P * t : 2 * P * (t + 1)].bitcast(E2M1),
                lhsT_scale=wu_sc[a][:, P * t : P * (t + 1)],
                rhs=got_w[c][:, cols].bitcast(E4M3), rhs_scale=got_sc[c][:, cols],
                start=True, stop=True,
            )

        def down_matmuls(out, t, words, scales):
            nc.tensor.matmul_mx(
                out, lhsT=wd8[:, P * t : P * (t + 1)].bitcast(E4M3), lhsT_scale=wd_sc[UPPER_ROW:P, P * t : P * (t + 1)],
                rhs=words[0].bitcast(E4M3), rhs_scale=scales[0], start=True, stop=False,
            )
            nc.tensor.matmul_mx(
                out, lhsT=wd4[:, 2 * P * t : 2 * P * (t + 1)].bitcast(E2M1), lhsT_scale=wd_sc[:, P * t : P * (t + 1)],
                rhs=words[1].bitcast(E4M3), rhs_scale=scales[1], start=False, stop=True,
            )

        def quantize_h(words, scales, woven_h):
            nc.vector.quantize_mx(
                out=words.rearrange("p a j -> p (a j)").bitcast(E4M3),
                scales=scales.rearrange("p a j -> p (a j)"),
                in_=woven_h.rearrange("p a j t -> p (a j t)"),
            )

        acts = {}
        h_pairs = {}
        h_in = {}
        y = {}

        def gelu_pair(c, a, u, b, on=None):
            bank = bank_tile([P, 2, CH], b)
            for e in range(2):
                up_matmul(bank[:, e, :], c, a, 2 * u + e, slice(0, CH))
            acts[c, a, u] = kept([P, 2, CH], F32, "act%d%d%d" % (c, a, u), on)[:]
            nc.scalar.activation(acts[c, a, u], bank[:], GELU)

        def scale_planes(c, a):
            h_pairs[c, a] = kept([P, 2, CH, 2], BF16, "h_pairs%d%d" % (c, a))
            for t in SCALE_ORDER:
                u, e = divmod(t, 2)
                nc.scalar.activation(h_pairs[c, a][:, u, :, e], acts[c, a, u][:, e, :], COPY, scale=sm_sb[:, a, t : t + 1])

        y_high = kept([P, 2, LAST * CH], F32, "y_high")

        def high_pair(c):
            return y_high[:, :, (c - 1) * CH : c * CH]

        def empty_low(c, bank):
            low = kept([P, 2, CH], F32, "y_low%d" % c)
            nc.scalar.copy(low[:], bank[:])
            y[c] = [low[:, 0, :], low[:, 1, :], high_pair(c)[:, 0, :], high_pair(c)[:, 1, :]]

        def weave_hidden(c, a):
            nc.scalar.copy(
                h_in[c][:, a].rearrange("p j t -> p (j t)").bitcast(F32).rearrange("p (j u) -> p j u", u=2),
                h_pairs[c, a][:].rearrange("p u j e -> p u (j e)").bitcast(F32).rearrange("p u j -> p j u"),
            )

        def codes_place(c):
            return "total02" if c == 1 else "h_w%d" % c

        def down(c):
            h_w = kept([P, 2, CH], U32, "h_w%d" % c, codes_place(c))
            h_sc = ring.tile([P, 2, CH], U8, name="h_sc", tag="h_sc", align_bytes=64)
            quantize_h(h_w[:], h_sc[:], h_in[c][:])
            banks = [bank_tile([P, 2, CH], 6 + u) for u in range(2)]
            for t in range(4):
                for half in range(2):
                    cols = slice(P * half, P * (half + 1))
                    down_matmuls(
                        banks[t // 2][:, t % 2, cols], t,
                        [h_w[:, a, cols] for a in range(2)], [h_sc[:, a, cols] for a in range(2)],
                    )
            return banks

        gather_table(got_sc, tab_sc, 0, NCH, kept([P, J], U8, "got_sc0"))
        gather_table(got_w, tab_w, 0, 1, kept([P, CH], U32, "got_w0"))
        for a in range(2):
            deal(wu[a][:].bitcast(U16), wu_raw[:].bitcast(U16)[:, PASS * a : PASS * (a + 1)])
        gather_table(got_w, tab_w, 1, LAST, kept([P, LAST * CH], U32, "got_w1"))
        for a in range(2):
            deal(wu_sc[a][:], wu_sc_raw[:, PASS * a : PASS * (a + 1)])
        act_first = {}
        for a in range(2):
            for half in range(2):
                act_first[half, a] = kept([P, P, 4], F32, "act_first%d%d" % (half, a))
                bank = bank_tile([P, 4, P], 2 * a + half)
                for t in range(4):
                    up_matmul(bank[:, t, :], 0, a, t, slice(P * half, P * (half + 1)))
                nc.scalar.activation(act_first[half, a][:], bank[:].rearrange("p t j -> p j t"), GELU)
        wd8 = kept([P, N], I32, "wd8")
        wd4 = kept([P, 2 * N], U8, "wd4")
        nc.gpsimd.tensor_copy(
            wd8[:].rearrange("p (t m i) -> p m t i", t=4, i=4), wd8_raw[:].rearrange("p (m i t) -> p m t i", t=4, i=4)
        )
        deal(wd4[:].bitcast(U16), wd4_raw[:].bitcast(U16))
        wd_sc = kept([P, N], U8, "wd_sc")
        deal(wd_sc[:], wd_sc_raw[:])
        first_high = bank_tile([P, 2, CH], 5)
        first_planes = [bank_tile([P, CH], 6)[:], bank_tile([P, CH], 4)[:], first_high[:, 0, :], first_high[:, 1, :]]
        h_first = [kept([P, 2, P, 4], BF16, "h_first0"), laid([P, 2, P, 4], BF16, "h_first1", H_FIRST_AT)]
        h_w_first = [kept([P, 2, P], U32, "h_w_first%d" % a) for a in range(2)]
        h_sc_first = [kept([P, 2, P], U8, "h_sc_first%d" % a) for a in range(2)]

        def first_product(a, half):
            factors = sm_sb[:, a, :].unsqueeze(1).to_broadcast([P, P, 4])
            nc.vector.tensor_tensor(h_first[a][:, half], act_first[half, a][:], factors, MULT)

        def first_quantize(a, halves):
            quantize_h(h_w_first[a][:, halves], h_sc_first[a][:, halves], h_first[a][:, halves])

        first_product(0, 0)
        first_product(0, 1)
        first_product(1, 0)
        first_quantize(0, slice(0, 2))
        first_product(1, 1)
        first_quantize(1, slice(0, 1))
        first_quantize(1, slice(1, 2))
        for t in range(4):
            for half in range(2):
                down_matmuls(
                    first_planes[t][:, P * half : P * (half + 1)], t,
                    [h_w_first[a][:, half, :] for a in range(2)], [h_sc_first[a][:, half, :] for a in range(2)],
                )
        first_res = laid([P, CH], F32, "first_res", FIRST_RES_AT)
        nc.vector.tensor_copy(first_res[:], res[0][:].indirect(picks(0)))
        first_y1 = kept([P, CH], F32, "first_y1")
        first_y_high = kept([P, 2, CH], F32, "first_y_high")
        y[0] = {1: first_y1[:], 2: first_y_high[:, 0, :], 3: first_y_high[:, 1, :]}
        nc.scalar.copy(first_y1[:], first_planes[1])
        nc.scalar.copy(first_y_high[:], first_high[:])

        h_in[1] = kept([P, 2, CH, 4], BF16, "h_in1")
        gelu_pair(1, 0, 0, 0)
        gelu_pair(1, 0, 1, 1)
        scale_planes(1, 0)
        gelu_pair(1, 1, 0, 4)
        weave_hidden(1, 0)
        gelu_pair(1, 1, 1, 5)
        scale_planes(1, 1)
        gelu_pair(2, 0, 0, 0, "act110")
        weave_hidden(1, 1)
        pages[1] = laid([P, T], F32, "page1", PAGE1_AT)
        pages[2] = kept([P, T], F32, "page2", "h_w_first1")
        pages[3] = kept([P, T], F32, "page3", "h_sc_first1")
        for t in (1, 2, 3):
            nc.gpsimd.memset(pages[t][:], 0.0)

        def add_residual(c, t, total):
            if (c, t) == (0, 0):
                nc.vector.tensor_tensor(total, first_planes[0], first_res[:], ADD)
            else:
                nc.vector.tensor_tensor(total, res[t][:].indirect(picks(c)), y[c][t], ADD)

        def scatter(c, t, total):
            nc.vector.tensor_tensor(pages[t][:].indirect(picks(c)), total, weights_of(c), MULT)

        out_planes = out_0.rearrange("(p t) c -> p t c", t=4)
        pairs = kept([P, 2, T, 2], BF16, "pairs")

        def finish_plane(t):
            nc.sync.dma_start(out_planes[:, t, :], pages[t][:])
            if t < 2:
                nc.scalar.copy(pairs[:, 0, :, t], pages[t][:])
            if t == 2:
                nc.scalar.copy(pairs[:, 1, 0:SPLIT], pages[t][:, 0:SPLIT].unsqueeze(2).to_broadcast([P, SPLIT, 2]))
                nc.scalar.copy(pairs[:, 1, SPLIT:T, 0], pages[t][:, SPLIT:T])

        def first_planes_of(c, count):
            totals = [
                kept([P, CH], F32, "total%d%d" % (c, t), "first_y_high" if (c, t) == (1, 0) else None)
                for t in range(count)
            ]
            add_residual(c, 0, totals[0][:])
            for t in range(count):
                if t < count - 1:
                    add_residual(c, t + 1, totals[t + 1][:])
                scatter(c, t, totals[t][:])

        def after_weave(c):
            return kept([P, CH], F32, "late%d" % c, "h_pairs%d1" % c)

        def next_hidden(c, banks):
            gelu_pair(c, 0, 1, 1, "act%d11" % (c - 1))
            scale_planes(c, 0)
            gelu_pair(c, 1, 0, 2, None if c < LAST else "h_pairs%d0" % (c - 1))
            empty_low(c - 1, banks[0])
            nc.scalar.copy(high_pair(c - 1), banks[1][:])
            h_in[c] = kept([P, 2, CH, 4], BF16, "h_in%d" % c, codes_place(c - 1))
            weave_hidden(c, 0)
            gelu_pair(c, 1, 1, 6)
            scale_planes(c, 1)
            if c < LAST:
                gelu_pair(c + 1, 0, 0, 0, "act%d10" % c)
            weave_hidden(c, 1)

        for c in range(LAST):
            before = 3 if c == 0 else 2
            first_planes_of(c, before)
            banks = down(c + 1)
            if c + 1 < LAST:
                next_hidden(c + 2, banks)
            else:
                empty_low(LAST, banks[0])
                nc.scalar.copy(high_pair(LAST), banks[1][:])
            late = after_weave(c + 1)
            add_residual(c, before, late[:])
            scatter(c, before, late[:])
        last = kept([P, 5 * CH], F32, "last")
        long_total = last[:, 0 : LAST * CH]
        last_totals = [last[:, (2 + t) * CH : (3 + t) * CH] for t in range(3)]
        for t in (0, 1):
            add_residual(LAST, t, last_totals[t])
        scatter(LAST, 0, last_totals[0])
        finish_plane(0)
        add_residual(LAST, 2, last_totals[2])
        scatter(LAST, 1, last_totals[1])
        finish_plane(1)
        nc.vector.tensor_tensor(long_total, res[3][:].indirect(picks(1, LAST)), y_high[:, 1, :], ADD)
        scatter(LAST, 2, last_totals[2])
        finish_plane(2)
        nc.vector.tensor_tensor(pages[3][:].indirect(picks(1, LAST)), long_total, weights_of(1, LAST), MULT)
        finish_plane(3)

        out_w = kept([P, T], U32, "out_w")
        out_sc = kept([P, T // 2], U8, "out_sc")
        out_words = out_1[0].rearrange("p t i -> p (t i)").bitcast(I32)
        pair_words = pairs[:].rearrange("p u c e -> p u (c e)").bitcast(F32)
        woven = {}

        def round_last_plane(copy, lo, hi):
            copy(pairs[:, 1, lo:hi, 1], pages[3][:, lo:hi])

        def weave_out(copy, lo, hi):
            woven[lo] = kept([P, hi - lo, 4], BF16, "woven%d" % lo)
            words = woven[lo][:].rearrange("p c t -> p (c t)").bitcast(F32).rearrange("p (c u) -> p c u", u=2)
            copy(words, pair_words[:, :, lo:hi].rearrange("p u c -> p c u"))

        def quantize_out(lo, hi):
            side = lo // (T // 2)
            nc.vector.quantize_mx(
                out=out_w[:, lo:hi].bitcast(E4M3),
                scales=out_sc[UPPER_ROW * side : P, lo - side * T // 2 : hi - side * T // 2],
                in_=woven[lo][:].rearrange("p c t -> p (c t)"),
            )

        vector_pieces = ((0, 512), (512, SPLIT))
        scalar_pieces = ((SPLIT, 1536), (1536, 1792), (1792, T))
        for piece in vector_pieces:
            round_last_plane(nc.vector.tensor_copy, *piece)
        round_last_plane(nc.scalar.copy, SPLIT, 1536)
        round_last_plane(nc.scalar.copy, 1536, T)
        for piece in scalar_pieces:
            weave_out(nc.scalar.copy, *piece)
        for piece in vector_pieces:
            weave_out(nc.vector.tensor_copy, *piece)
        for lo, hi in vector_pieces + scalar_pieces:
            quantize_out(lo, hi)
            nc.sync.dma_start(out_words[:, lo:hi], out_w[:, lo:hi].bitcast(I32))
        for q in range(4):
            queue = nc.scalar if q < 3 else nc.sync
            rows = out_2[0, 4 * q : 4 * q + 4, :].bitcast(I32).rearrange("r (side c) -> side r c", side=2)
            queue.dma_start(rows, out_sc[32 * q : 32 * q + 2 * UPPER_ROW, :].bitcast(I32))
